import numpy as np, ml_dtypes
CORES = [9,25,41,57]
N = 4
BF = ml_dtypes.bfloat16
W, H, Q, L, V, TH, TH2 = 4096, 256, 16, 4, 8, 2345, 820
J = Q - L + 1
HALF = (J - 1) // 2
B = HALF + L - 1
def which(s, z):
    return np.maximum(1, np.add.reduce((s <= z[:, None, :]).astype(np.int64), axis=1)) - 1
def place(s, c, k, p):
    sk = np.take_along_axis(s, k[:, None, :], 1); ck = np.take_along_axis(c, k[:, None, :], 1)
    return ((p - sk) * (2 * ck + 1) + 37 * ck) & (W - 1)
def pick(x, f):
    return np.take_along_axis(x, f.reshape(8, 1, -1), 2).reshape(8, 16, -1, H)
def seen(x, s, c, z):
    o = (5 * np.arange(H)) & (H - 1); got = []
    for q in range(N):
        so = s[q][..., o]; co = c[q][..., o]
        got.append(pick(x[q], place(so, co, which(so, z[q]), z[q][:, None, :] + np.arange(Q)[None, :, None] - B)))
    return np.stack(got)
def parts(rng):
    span = rng.integers(116, 141, (N, 8, 1, 1))
    x = 128 + np.floor((rng.random((N, 8, 16, W), dtype=np.float32) - 0.5) * span).astype(np.int64)
    tm = 128 + np.floor((rng.random((N, 8, 16, L, H)) - 0.5) * span[..., None]).astype(np.int64)
    s = np.sort(rng.integers(0, W, (N, 8, 16, H)), axis=2); c = rng.integers(0, 1024, (N, 8, 16, H)); z = rng.integers(16, 3001, (N, 8, H))
    return x, s, c, z, tm
def pack(x, s, c, z, tm):
    return {"xl": np.ascontiguousarray(x).reshape(N, 128, W).astype(np.float32).astype(BF), "s0": np.ascontiguousarray(s).reshape(N, 128, H).astype(np.int32),
            "cf": np.ascontiguousarray(c).reshape(N, 128, H).astype(np.int32), "z0": np.ascontiguousarray(z).astype(np.int32),
            "t0": np.ascontiguousarray(tm).reshape(N, 128, L * H).astype(np.float32).astype(BF)}
def setup_inputs(rng):
    return pack(*parts(rng))
def setup_inputs_spread(rng):
    amps = np.array([4, 16, 32, 64, 96, 128])
    x = np.clip(128 + np.floor((2 * rng.random((N, 8, 16, W), dtype=np.float32) - 1) * rng.choice(amps, (N, 8, 1, W))), 0, 255).astype(np.int64)
    tm = np.clip(128 + np.floor((2 * rng.random((N, 8, 16, L, H)) - 1) * rng.choice(amps, (N, 8, 1, L, H))), 0, 255).astype(np.int64)
    s = np.where(rng.random((N, 8, 1, H)) < 0.5, rng.integers(0, W, (N, 8, 16, H)), np.clip(np.floor(np.exp2(12 * rng.random((N, 8, 16, H)))).astype(np.int64) - 1, 0, W - 1))
    c = np.clip(np.floor(np.exp2(10 * rng.random((N, 8, 16, H)))).astype(np.int64) - 1, 0, 1023)
    z = np.where(rng.random((N, 8, H)) < 0.5, rng.integers(16, 3001, (N, 8, H)), np.clip(np.floor(np.exp2(11.6 * rng.random((N, 8, H)))).astype(np.int64), 16, 3000))
    return pack(x, np.sort(s, axis=2), c, z, tm)
def turns(w, u):
    return np.where((u & 1) == 1, 255 - w, w)
def setup_inputs_ends(rng):
    x = 255 * (rng.random((N, 8, 16, W), dtype=np.float32) < 0.125).astype(np.int64); tm = 255 * (rng.random((N, 8, 16, L, H)) < 0.125).astype(np.int64)
    flip = rng.permutation(np.array([0, 0, 1, 1]))
    for g in range(2, 6):
        if flip[g - 2] == 1: x[:, g] = 255 - x[:, g]; tm[:, g] = 255 - tm[:, g]
    nz = rng.integers(0, 17, (N, 8, 1, H)); low = np.where(np.arange(16).reshape(1, 1, 16, 1) < nz, 0, W - 1)
    s = np.where(rng.random((N, 8, 1, H)) < 0.5, low, (W - 1) * rng.integers(0, 2, (N, 8, 16, H))); s[..., 0] = 0; s[..., H - 1] = W - 1
    c = 1023 * rng.integers(0, 2, (N, 8, 16, H)); z = 16 + 2984 * rng.integers(0, 2, (N, 8, H)); z[..., 0] = 16; z[..., H - 1] = 3000
    level = 255 * int(rng.integers(0, 2)); turn = int(rng.integers(0, 2))
    x[:, 7] = level; rec = 255 * rng.integers(0, 2, (N, 1, 1, H)); rec[..., 0] = 255 - level; rec[..., H - 1] = 255 - level; rec[..., 1] = level; rec[..., H - 2] = level; tm[:, 7] = rec
    for q in range(N): x[q, 0] = 255 * ((q + turn) % 2)
    tm[:, 0] = 255 * rng.integers(0, 2, (N, 1, 1, H))
    x[:, 1, :, 0::2] = 0; x[:, 1, :, 1::2] = 255; tm[:, 1] = 255 * rng.integers(0, 2, (N, 1, L, H))
    code = 255 * rng.integers(0, 2, (16, HALF * N))
    for q in range(N): x[q, 6] = code[:, (np.arange(W) - HALF * q) % (HALF * N)]
    s[:, 6] = 0; c[:, 6] = 0
    b = int(rng.integers(0, N)); s[:, 5] = W - 1; c[:, 5] = 1023; z[:, 5] = 3000; z[b, 5] = 16
    u = np.arange(W) - 4300; col = (u * 2047 + 37 * 1023) & (W - 1)
    far = W - 1 + HALF * (V - 1 - (V - 1) // N)
    p = 255 * rng.integers(0, 2, (16, 1)); other = np.where(rng.permutation(16).reshape(16, 1) < 8, 255 - p, p)
    period = HALF * (N - 1); ring = 255 * rng.integers(0, 2, (16, period)); ring[:, int(u[np.argmin(col)]) % period] = (255 - turns(p, far - HALF))[:, 0]
    for d in range(N):
        near = turns(p if d % 2 == 0 else other, u)
        if d == N - 1: near = np.where((u >= -far - HALF) & (u < -far - HALF + L), turns(p, u), near)
        x[(b + d) % N, 5][:, col] = np.where(u < -2600, near, ring[:, (u + HALF * d) % period])
    y = seen(x, s, c, z)
    tm[:, 6] = y[:, 6, :, J - 1:J - 1 + L]; tm[:, 5] = y[:, 5, :, :L]; tm[b, 5] = turns(other, np.arange(L))[:, :, None]
    return pack(x, s, c, z, tm)
def setup_inputs_corners(rng):
    x, s1, c, z, tm = parts(rng); gs = rng.permutation(8)
    x[:, gs[0]] = 120 + (x[:, gs[0]] & 15); x[:, gs[1]] = rng.integers(0, 256, (N, 16, W))
    kind = rng.integers(0, 8, (N, 8, 1, H)); s = np.where(kind == 1, s1[:, :, 5:6], s1); s = np.where(kind == 2, s1[:, :, ::-1], s); s = np.where(kind == 3, W - 1, s)
    s = np.where(kind == 4, np.arange(16).reshape(1, 1, 16, 1), s); s = np.where(kind == 5, rng.permuted(s1, axis=2), s)
    c = np.where(rng.random((N, 8, 16, H)) < 0.3, rng.choice(np.array([0, 1, 511, 512, 1023]), (N, 8, 16, H)), c)
    so = s[..., (5 * np.arange(H)) & (H - 1)]; near = np.take_along_axis(so, rng.integers(0, 16, (N, 8, 1, H)), 2)[:, :, 0]
    z = np.clip(near + rng.choice(np.array([-6, -1, 0, 1, 5, Q - 1, Q, Q + 1]), (N, 8, H)), 16, 3000)
    y = seen(x, s, c, z); j0 = rng.choice(np.array([0, 1, HALF, J - 1]), (N, 8, 1, 1, H)); m = np.take_along_axis(y, j0 + np.arange(L).reshape(1, 1, 1, L, 1), 3)
    tm = np.where(rng.random((N, 8, 1, 1, H)) < 0.6, m, tm)
    tm[:, gs[2]] = 255 * rng.integers(0, 2, (N, 1, L, H)); tm[:, gs[3]] = m[:, gs[3]]
    tm[:, gs[4]] = 255 * rng.integers(0, 2, (N, 1, L, H)); tm[:, gs[4], :, :, H - 1] = m[:, gs[4], :, :, H - 1]
    return pack(x, s, c, z, tm)
def steps(rng):
    b = TH2 // 16; e = rng.integers(-8, 9, 8)
    return b + np.concatenate([e, -e]) + (np.arange(16) < TH2 - 16 * b).astype(np.int64)
def pairs(rng, total, w):
    a = np.zeros(16, np.int64); a[[0, 9]] = (w + 1) // 2; a[[1, 8]] = w // 2
    rest = total - 2 * w; b = rest // 12; e = rng.integers(-8, 9, 6)
    a[[2, 3, 4, 5, 6, 7, 10, 11, 12, 13, 14, 15]] = b + np.concatenate([e, -e]) + (np.arange(12) < rest - 12 * b).astype(np.int64)
    return a
def setup_inputs_edges(rng):
    x, s, c, z, tm = parts(rng)
    for g in range(8):
        if g % 4 == 1: continue
        p0 = rng.integers(50, 71, 16); p1 = p0 + steps(rng); p2 = p1 + steps(rng); p3 = p2 - steps(rng); p3[int(rng.integers(0, 16))] -= 1
        p = np.stack([p0, p1, p2, p3], axis=1)
        for q in range(N): x[q, g] = p[:, (np.arange(W) + int(rng.integers(0, 4))) & 3]
    w = 257 + 4 * int(rng.integers(0, 6)); p0 = rng.integers(20, 61, 16); p1 = p0 + pairs(rng, TH2 + 1, w); p2 = p1 + rng.integers(1, 4, 16); p3 = p2 - pairs(rng, TH2, w + 2)
    p = np.stack([p0, p1, p2, p3], axis=1)
    for q in range(N): x[q, 5] = p[:, (np.arange(W) + int(rng.integers(0, 4))) & 3]
    y = seen(x, s, c, z); dist = rng.choice(np.array([0, TH - 1, TH, TH + 1]), (N, 8, 1, 1, H)); j0 = rng.integers(0, 4, (N, 8, 1, 1, H))
    m = np.take_along_axis(y, j0 + np.arange(L).reshape(1, 1, 1, L, 1), 3); each = dist // (16 * L)
    d = each + (np.arange(16 * L).reshape(1, 1, 16, L, 1) < dist - 16 * L * each)
    sign = np.where(m < 80, -1, np.where(m > 135, 1, 1 - 2 * (np.arange(16).reshape(1, 1, 16, 1, 1) & 1)))
    planted = (np.arange(8) % 4 != 1).reshape(1, 8, 1, 1, 1)
    return pack(x, s, c, z, np.where(planted, m + sign * d, tm))
def check_inputs(d):
    bad = []
    for k, lo, hi in (("xl", 0, 255), ("s0", 0, W - 1), ("cf", 0, 1023), ("z0", 16, 3000), ("t0", 0, 255)):
        a = np.asarray(d[k]).astype(np.float64)
        if not (np.min(a) >= lo and np.max(a) <= hi): bad.append("range of " + k)
        elif np.any(a != np.floor(a)): bad.append("whole numbers in " + k)
    return bad
def reference(xl, s0, cf, z0, t0):
    x = xl.astype(np.int32).reshape(N, 8, 16, W); s = s0.astype(np.int64).reshape(N, 8, 16, H); c = cf.astype(np.int64).reshape(N, 8, 16, H)
    z = z0.astype(np.int64); tm = t0.astype(np.int32).reshape(N, 8, 16, L, H); ties = np.zeros((N, 8), np.int64)
    row = np.arange(16)[None, :, None]; m = np.arange(Q)[None, :, None]
    for t in range(V):
        for r in range(N):
            q = (r + t) % N
            o = ((5 * np.arange(H)[None, :] + ties[r][:, None]) & (H - 1))[:, None, :]
            so = np.take_along_axis(s[q], o, 2); co = np.take_along_axis(c[q], o, 2)
            k = which(so, z[r])
            y = pick(x[q], place(so, co, k, z[r][:, None, :] + m - B))
            e = np.stack([np.add.reduce(np.abs(y[:, :, j:j + L] - tm[r]), axis=(1, 2)) for j in range(J)])
            best = np.argmin(e, axis=0); tie = np.min(e, axis=0) < TH
            so = so + np.where(tie[:, None, :] & (row >= k[:, None, :]), HALF - best[:, None, :], 0)
            np.put_along_axis(s[q], o, so, 2)
            zz = np.where(tie, z[r], np.maximum(z[r] - Q, 0)); k = np.where(tie, k, which(so, zz))
            v = pick(x[q], place(so, co, k, zz[:, None, :] + m))
            over = (np.add.reduce(np.abs(v[:, :, 1:] - v[:, :, :-1]), axis=1) > TH2)[:, L - 1:]
            n = np.where(np.any(over, axis=1), L + np.argmax(over, axis=1), Q)
            tm[r] = np.take_along_axis(v, n[:, None, None, :] - L + np.arange(L)[None, None, :, None], 2)
            z[r] = zz + n - 1
            ties[r] = np.add.reduce(tie.astype(np.int64), axis=1)
    return {"ys": s.reshape(N, 128, H).astype(np.float32), "yz": z.astype(np.float32), "yt": tm.reshape(N, 128, L * H).astype(np.float32).astype(BF)}

@@ -1,0 +1,531 @@
+import numpy as np
+from concourse.mybir import dt, AluOpType as Op, ActivationFunctionType as AF
+
+NV = 8
+J = 13
+J0 = 9
+NM = 4
+GP = 2
+MAGIC = 201326592.0
+EARLY, LATE = 37528.0, 1.0e9
+
+F32, BF, F16, I32, U16 = "float32", "bfloat16", "float16", "int32", "uint16"
+SCRATCH = {
+    "x": ("sbuf", [128, 4096], BF), "t0s": ("sbuf", [128, 1024], BF), "ytb": ("sbuf", [128, 1024], BF),
+    "s0s": ("sbuf", [128, 256], I32), "cfs": ("sbuf", [128, 256], I32), "z0s": ("sbuf", [8, 256], I32), "z0f": ("sbuf", [8, 256], F32),
+    "st0": ("sbuf", [128, 256], F32), "st1": ("sbuf", [128, 256], F32), "sg": ("sbuf", [128, 256], F32),
+    "dg0": ("sbuf", [128, 256], F32), "dg1": ("sbuf", [128, 256], F32), "ysb": ("sbuf", [128, 256], F32),
+    "zb": ("sbuf", [128, 256], F32), "zl": ("sbuf", [128, 8 * 256], F32), "zm": ("sbuf", [128, 8 * 256], F32),
+    "al": ("sbuf", [128, 64], F32), "am": ("sbuf", [128, 64], F32),
+    "li": ("sbuf", [128, 16], I32), "lm": ("sbuf", [128, 16], I32), "lu": ("sbuf", [128, 16], U16),
+    "iP": ("sbuf", [128, 128], I32), "iQ": ("sbuf", [128, 128], I32), "iC": ("sbuf", [128, 104], I32), "iJ": ("sbuf", [128, 104], I32),
+    "iL": ("sbuf", [128, 16], I32), "i64": ("sbuf", [128, 32], I32),
+    "pg": ("sbuf", [128, 128], I32), "qg": ("sbuf", [128, 128], I32), "pm": ("sbuf", [128, 128], I32), "qm": ("sbuf", [128, 128], I32),
+    "sh": ("sbuf", [128, 32], I32), "q1": ("sbuf", [128, 32], I32), "q2": ("sbuf", [128, 32], I32), "l5": ("sbuf", [128, 16], I32),
+    "w9": ("sbuf", [128, 128], F32), "w18": ("sbuf", [128, 128], F32), "mu": ("sbuf", [128, 32], F32), "shf": ("sbuf", [128, 8], F32),
+    "gf": ("sbuf", [128, 8], F32), "gr": ("sbuf", [128, 104], F32), "sg1": ("sbuf", [128, 104], F32), "sg2": ("sbuf", [128, 104], F32),
+    "B32": ("sbuf", [128, 128], F32), "Bb": ("sbuf", [128, 128], BF), "Ib": ("sbuf", [128, 128], BF), "I16": ("sbuf", [128, 128], BF),
+    "Im": ("sbuf", [128, 128], BF), "Ih": ("sbuf", [128, 128], F16), "W0": ("sbuf", [128, 128], F16), "W1": ("sbuf", [128, 128], F16),
+    "Wu": ("sbuf", [128, 512], BF), "G1": ("sbuf", [128, 8], BF), "G32": ("sbuf", [128, 8], BF), "Z": ("sbuf", [128, 8, 32], BF),
+    "RT": ("sbuf", [128, 104], BF), "cj": ("sbuf", [128, 104], BF), "cpad": ("sbuf", [128, 104], BF), "KD": ("sbuf", [128, 104], F32),
+    "ONE": ("sbuf", [128, 104], F32), "RD": ("sbuf", [128, 256], BF), "Qc": ("sbuf", [128, 32], F16), "rp1": ("sbuf", [128, 8], F32),
+    "LB": ("sbuf", [128, 16], F32), "LF": ("sbuf", [128, 16], F32), "R8": ("sbuf", [8, 128], F32),
+    "w7": ("sbuf", [128, 128], BF), "c185": ("sbuf", [128, 128], BF), "cm16": ("sbuf", [128, 128], BF), "c3": ("sbuf", [128, 128], BF),
+    "c205": ("sbuf", [128, 8], BF),
+    "yps": ("psum", [128, 128, 16], F32), "dif": ("psum", [128, 512], F32), "vt": ("psum", [128, 512], F32),
+    "kb": ("psum", [128, 512], F32), "sm": ("psum", [128, 512], F32),
+}
+_HALF = {"cmp": (128, BF), "geb": (128, BF), "Hb": (128, F32), "oH": (128, F32), "oD": (128, F16), "fi": (128, I32), "fm": (128, I32),
+         "of": (128, U16), "y2": (2048, BF), "v2": (2048, BF), "Va": (1536, BF), "ks": (104, F32), "rr": (8, F32), "dd": (8, F32),
+         "Xs": (256, BF), "Xr": (256, BF), "dge": (128, F32), "zp": (128, F32), "nx": (104, F32), "ns": (104, F32), "Xn": (128, BF),
+         "Xnr": (128, BF), "nsb": (128, BF), "tof": (32, U16), "Ma": (512 * (J - J0), BF)}
+for _n, (_c, _d) in _HALF.items():
+    SCRATCH[_n] = ("sbuf", [128, 2 * _c], _d)
+for _m in range(NM):
+    SCRATCH["mb%d" % _m] = ("sbuf", [128, 128, 4], BF)
+SCRATCH["ts"] = ("sbuf", [128, NV * 1024], BF)
+for _t in range(NV + 1):
+    SCRATCH["tl%d" % _t] = ("sbuf", [128, 256, 4], BF)
+SEMAPHORES = ["v", "a", "p", "q", "lx", "ls", "lc", "lz", "lt", "loc", "sto"]
+for _t in range(1, NV + 1):
+    SEMAPHORES += ["rA%d" % _t, "rz%d0" % _t, "rz%d1" % _t, "rT%d0" % _t, "rT%d1" % _t]
+SEMAPHORES.remove("rA%d" % NV)
+
+
+def build(T, gs, nxt):
+    ops, lastw, readers, accs = [], {}, {}, {}
+
+    def add(eng, fns, cost, rd=(), wr=(), acc=None, acq=None, use=None, after=(), pin=None):
+        i = len(ops)
+        deps = {}
+        for k in rd:
+            for o in ([lastw[k]] if k in lastw else []) + accs.get(k, []):
+                deps[o] = True
+            readers.setdefault(k, []).append(i)
+        if acc is not None:
+            deps[lastw[acc]] = deps.get(lastw[acc], False)
+            accs.setdefault(acc, []).append(i)
+        for k in wr:
+            for o in readers.get(k, []) + ([lastw[k]] if k in lastw else []) + accs.get(k, []):
+                if o != i:
+                    deps[o] = deps.get(o, False)
+            lastw[k], readers[k], accs[k] = i, [], []
+        for o in after:
+            deps[o] = deps.get(o, False)
+        if acq is not None:
+            use = i
+        ops.append(dict(eng=eng, fns=fns, cost=cost, deps=deps, acq=acq, use=use, sym=pin))
+        return i
+
+    v, s, p, g = gs["v"], gs["a"], gs["p"], gs["q"]
+
+    def V(fn, c, rd=(), wr=(), **kw):
+        return add("v", [fn], 0.05 + max(64, c) * 0.001, rd, wr, **kw)
+
+    def A(fn, c, rd=(), wr=(), **kw):
+        return add("a", [fn], 0.065 + c * 0.001, rd, wr, **kw)
+
+    def P(fns, c, rd=(), wr=(), **kw):
+        return add("p", fns, c * 0.0006, rd, wr, **kw)
+
+    def mm(out, l, r, start=True, stop=True):
+        return lambda last: p.matmul(out, l, r, start, stop or last)
+
+    def ts(out, a, s1, s2, o0, o1=None):
+        if o1 is None:
+            return lambda last: v.tensor_scalar(out, a, s1, None, o0)
+        return lambda last: v.tensor_scalar(out, a, s1, s2, o0, o1)
+
+    def tt(out, a, b, o):
+        return lambda last: v.tensor_tensor(out, a, b, o)
+
+    def cp(out, a):
+        return lambda last: v.tensor_copy(out, a)
+
+    def act(out, a, f=AF.Copy, bias=0.0, scale=1.0):
+        return lambda last: s.activation(out, a, f, bias=bias, scale=scale)
+
+    def scan(out, a, b, o0, o1):
+        return lambda last: v.tensor_tensor_scan(out, a, b, 0.0, o0, o1)
+
+    def load(out, a, sem, key, lat):
+        return add("d", [lambda last: gs["d"].dma_start(out, a)], lat, (), [key], pin=(sem, 16))
+
+    def H(name, h, a=0, b=None, step=None):
+        n = _HALF[name][0]
+        return T[name][:, n * h + a: n * h + (n if b is None else b): (step or 1)]
+
+    load(T.z0s[:, :], T.z0[:, :], "lz", "z0s", 2.5)
+    load(T.s0s[:, :], T.s0[:, :], "ls", "s0s", 3.0)
+    load(T.cfs[:, :], T.cf[:, :], "lc", "cfs", 3.5)
+    load(T.x[:, :], T.xl[:, :], "lx", "x", 9.0)
+    load(T.t0s[:, :], T.t0[:, :], "lt", "t0s", 10.0)
+
+    def iota(name, pat, base, cm):
+        add("q", [lambda last: g.iota(T[name][:, :], pat, base, cm)], 0.4, (), [name])
+    iota("iP", [[0, 128]], 0, 1)
+    iota("iQ", [[1, 128]], 0, 0)
+    iota("iL", [[16, 16]], 0, 0)
+    iota("iC", [[1, 8], [0, 13]], 0, 0)
+    iota("iJ", [[0, 8], [1, 13]], 0, 0)
+    iota("i64", [[64, 32]], -3, 0)
+
+    def C(fn, c, rd, wr):
+        return V(fn, c, rd, [wr])
+
+    def fill(name, val, c):
+        C(lambda last: v.memset(T[name][:, :], val) if name != "Z" else v.memset(T.Z[:, :, :], val), c, [], name)
+    A0 = lambda n, a=0, b=None: T[n][:, a:b] if b is not None else T[n][:, :]
+    C(ts(A0("pm"), A0("iP"), 15, None, Op.bitwise_and), 128, ["iP"], "pm")
+    C(tt(A0("LB"), A0("iL"), A0("pm", 0, 16), Op.add), 16, ["iL", "pm"], "LB")
+    C(ts(A0("l5"), A0("LB"), 5.0, None, Op.mult), 16, ["LB"], "l5")
+    C(ts(A0("LF"), A0("LB"), 205.0, None, Op.mult), 16, ["LB"], "LF")
+    C(ts(A0("qg"), A0("iQ"), 4, None, Op.arith_shift_right), 128, ["iQ"], "qg")
+    C(ts(A0("pg"), A0("iP"), 4, None, Op.arith_shift_right), 128, ["iP"], "pg")
+    C(ts(A0("qm"), A0("iQ"), 15, None, Op.bitwise_and), 128, ["iQ"], "qm")
+    C(ts(T.rp1[:, 0:1], T.pm[:, 0:1], 1.0, None, Op.add), 1, ["pm"], "rp1")
+    C(tt(A0("B32"), A0("pg"), A0("qg"), Op.is_equal), 256, ["pg", "qg"], "B32")
+    C(tt(T.R8[:, :], T.iP[0:8, :], T.qg[0:8, :], Op.is_equal), 256, ["iP", "qg"], "R8")
+    A(act(A0("Bb"), A0("B32")), 128, ["B32"], ["Bb"])
+    C(tt(A0("Ib"), A0("iP"), A0("iQ"), Op.is_equal), 256, ["iP", "iQ"], "Ib")
+    A(act(A0("I16"), A0("Ib"), scale=16.0), 128, ["Ib"], ["I16"])
+    A(act(A0("Im"), A0("Ib"), scale=-1.0), 128, ["Ib"], ["Im"])
+    C(cp(A0("Ih"), A0("Ib")), 64, ["Ib"], "Ih")
+    C(ts(A0("w9"), A0("qm"), 9.5, None, Op.add), 128, ["qm"], "w9")
+    C(ts(A0("w18"), A0("qm"), 18.5, None, Op.add), 128, ["qm"], "w18")
+    C(tt(A0("W0"), A0("w9"), A0("B32"), Op.mult), 256, ["w9", "B32"], "W0")
+    C(tt(A0("W1"), A0("w18"), A0("B32"), Op.mult), 256, ["w18", "B32"], "W1")
+    C(tt(A0("gf"), T.pg[:, 0:8], T.iQ[:, 0:8], Op.is_equal), 16, ["pg", "iQ"], "gf")
+    C(cp(A0("G1"), A0("gf")), 8, ["gf"], "G1")
+    C(ts(A0("G32"), A0("gf"), 32.0, None, Op.mult), 8, ["gf"], "G32")
+    fill("Z", 0.0, 256)
+    for k in range(4):
+        C(ts(T.Z[:, :, 16 + k], A0("gf"), -16.0, None, Op.mult), 8, ["gf", "Z"], "Z")
+    C(ts(A0("cj"), A0("iJ"), 10.0, None, Op.add), 104, ["iJ"], "cj")
+    C(ts(A0("cpad"), A0("iJ"), 0.0, 1000.0, Op.is_equal, Op.mult), 104, ["iJ"], "cpad")
+    C(ts(A0("KD"), A0("iJ"), 0.0, LATE, Op.is_equal, Op.mult), 104, ["iJ"], "KD")
+    C(tt(A0("gr"), T.pg[:, 0:104], A0("iC"), Op.is_equal), 208, ["pg", "iC"], "gr")
+    C(ts(A0("sg1"), A0("iJ"), float(J0), 32.0, Op.is_ge, Op.mult), 104, ["iJ"], "sg1")
+    C(ts(A0("sg2"), A0("sg1"), -16.0, None, Op.add), 104, ["sg1"], "sg2")
+    C(tt(A0("RT"), A0("sg2"), A0("gr"), Op.mult), 208, ["sg2", "gr"], "RT")
+    C(ts(T.RD[:, 0:128], A0("qm"), 0.0, None, Op.is_gt), 128, ["qm"], "RD")
+    C(ts(T.RD[:, 128:256], A0("qm"), 0.0, None, Op.is_gt), 128, ["qm"], "RD2")
+    C(ts(A0("sh"), T.pm[:, 0:32], 2, None, Op.arith_shift_right), 32, ["pm"], "sh")
+    C(ts(A0("q1"), A0("sh"), 12.0, None, Op.mult), 32, ["sh"], "q1")
+    C(tt(A0("q2"), A0("q1"), T.pm[:, 0:32], Op.add), 64, ["q1", "pm"], "q2")
+    C(tt(A0("Qc"), A0("q2"), A0("i64"), Op.add), 64, ["q2", "i64"], "Qc")
+    for u in range(4):
+        C(ts(T.mu[:, 8 * u:8 * u + 1], T.sh[:, 0:1], float(u), None, Op.is_equal), 1, ["sh"], "mu%d" % u)
+        C(ts(T.Wu[:, 128 * u:128 * u + 128], A0("Ib"), T.mu[:, 8 * u:8 * u + 1], None, Op.mult), 64, ["Ib", "mu%d" % u], "Wu%d" % u)
+    fill("w7", 2.0 ** -7, 64)
+    fill("c185", -18.5, 64)
+    fill("cm16", -16.0, 64)
+    fill("c3", 3.0, 64)
+    fill("c205", 205.0, 8)
+    fill("ONE", 1.0, 104)
+    for h in range(2):
+        C((lambda h: lambda last: v.memset(H("Xs", h), 0.0))(h), 128, [], "Xs%d" % h)
+        C((lambda h: lambda last: v.memset(H("Xn", h), 0.0))(h), 64, [], "Xn%d" % h)
+
+    C(cp(T.z0f[:, :], T.z0s[:, :]), 256, ["z0s"], "z0f")
+    tx = P([mm(T.sm[:, 0:256], T.R8[:, :], T.z0f[:, :])], 1024, ["R8", "z0f"], ["sm"], acq="sm")
+    for h in range(2):
+        V(cp(T.zb[:, 128 * h:128 * h + 128], T.sm[:, 128 * h:128 * h + 128]), 128, ["sm"], ["z0%d" % h], use=tx)
+    C(cp(A0("st0"), A0("s0s")), 256, ["s0s"], "st0_0")
+    lastw["st0_1"] = lastw["st0_0"]
+    C(ts(A0("dg1"), A0("cfs"), 2.0, 1.0, Op.mult, Op.add), 256, ["cfs"], "dg1")
+    for h in range(2):
+        for a in range(4):
+            src = T.t0s[:, 256 * a + 128 * h:256 * a + 128 * h + 128]
+            dst = T.tl0[:, 128 * h:128 * h + 128, a]
+            if a < 2:
+                V(cp(dst, src), 64, ["t0s"], ["T0%d" % h] if a == 0 else ["T0%d_%d" % (h, a)])
+            else:
+                A(act(dst, src), 128, ["t0s"], ["T0%d_%d" % (h, a)])
+
+    mcount = [0]
+    tx_of = {}
+
+    def gatherlist(t):
+        if t == 0:
+            C(ts(A0("lm"), A0("l5"), 255, None, Op.bitwise_and), 16, ["l5"], "lm")
+        else:
+            b = T.al[:, 4 * t:4 * t + 1]
+            if t == 1:
+                V(ts(A0("li"), A0("LB"), b, None, Op.add), 16, ["LB", "A1"], ["li"])
+            else:
+                V(ts(A0("li"), A0("LB"), b, T.al[:, 4 * t - 4:4 * t - 3], Op.add, Op.subtract), 16, ["LB", "A%d" % t, "A%d" % (t - 1)], ["li"])
+            C(ts(A0("lm"), A0("li"), 255, None, Op.bitwise_and), 16, ["li"], "lm")
+        C(cp(A0("lu"), A0("lm")), 16, ["lm"], "lu")
+        st, dn, do = "st%d" % (t % 2), "dg%d" % (t % 2), "dg%d" % ((t + 1) % 2)
+        A(act(A0("sg"), T[st][:, :].indirect(T.lu[:, :])), 256 * 1.5, ["lu", st + "_0", st + "_1"], ["sg"])
+        A(act(A0(dn), T[do][:, :].indirect(T.lu[:, :])), 256 * 1.5, ["lu", do], [dn])
+
+    def zref(t, h):
+        return T.zb[:, 128 * h:128 * h + 128] if t == 0 else T.zl[:, 256 * (t - 1) + 128 * h:256 * (t - 1) + 128 * h + 128]
+
+    def select(t, h, W, tail):
+        hs, c0 = str(h), 128 * h
+        X = T.vt[:, 256 * h:256 * h + 128]
+        Y = T.vt[:, 256 * h + 128:256 * h + 256]
+        dn = "dg%d" % (t % 2)
+        OHS, OK = (Y, "vY") if tail == 0 else (X, "vX")
+        tx = P([mm(T.sm[:, 0:128], A0("Bb"), H("cmp", h))], 128, ["Bb", "cmp" + hs], ["cnt" + hs], acq="sm")
+        V(ts(OHS, T.sm[:, 0:128], 1.0, T.rp1[:, 0:1], Op.max, Op.is_equal), 128, ["cnt" + hs, "rp1"], [OK + hs], use=tx)
+        if tail == 0:
+            V(ts(H("geb", h), T.sm[:, 0:128], T.rp1[:, 0:1], None, Op.is_le), 128, ["cnt" + hs, "rp1"], ["geb" + hs], use=tx)
+        V(tt(H("oD", h), OHS, T[dn][:, c0:c0 + 128], Op.mult), 128, [OK + hs, dn], ["oD" + hs])
+        V(tt(H("oH", h), OHS, H("Hb", h), Op.mult), 128, [OK + hs, "Hb" + hs], ["oH" + hs])
+        tx = P([mm(T.sm[:, 0:128], A0("w7"), A0("c185"), True, False), mm(T.sm[:, 0:128], A0(W), H("oD", h), False, False),
+                mm(T.sm[:, 0:128], A0("B32"), H("oH", h), False, True)], 768, ["w7", "c185", W, "oD" + hs, "oH" + hs, "B32"], ["F" + hs], acq="sm")
+        V(cp(H("fi", h), T.sm[:, 0:128]), 128, ["F" + hs], ["fi" + hs], use=tx)
+        V(ts(H("fm", h), H("fi", h), 4095, None, Op.bitwise_and), 128, ["fi" + hs], ["fm" + hs])
+        V(cp(H("of", h), H("fm", h)), 128, ["fm" + hs], ["of" + hs])
+
+    def samples(h, buf):
+        hs, k = str(h), 128 // GP
+        for q in range(GP):
+            A(act(H(buf, h, 16 * k * q, 16 * k * q + 16 * k), T.x[:, :].indirect(H("of", h, k * q, k * q + k))), 16 * k * 1.5,
+              ["x", "of" + hs], [buf + hs + "_%d" % q])
+    YK = lambda b, h: [b + str(h) + "_%d" % q for q in range(GP)]
+
+    def front(t, h):
+        hs, c0 = str(h), 128 * h
+        X = T.vt[:, 256 * h:256 * h + 128]
+        dn = "dg%d" % (t % 2)
+        V(tt(X, zref(t, h), T.sg[:, c0:c0 + 128], Op.subtract), 256, ["z%d%d" % (t, h), "sg"], ["vX" + hs])
+        V(ts(H("cmp", h), X, 0.0, None, Op.is_ge), 128, ["vX" + hs], ["cmp" + hs])
+        V(tt(H("Hb", h), X, T[dn][:, c0:c0 + 128], Op.mult), 128, ["vX" + hs, dn], ["Hb" + hs])
+        select(t, h, "W0", 0)
+        samples(h, "y2")
+
+    def heavy(t, h):
+        hs = str(h)
+        tl = T["tl%d" % t][:, 128 * h:128 * h + 128, :]
+        ta = lambda a: T["tl%d" % t][:, 128 * h:128 * h + 128, a]
+        TK = ["T%d%d" % (t, h)] + (["T0%d_%d" % (h, a) for a in (1, 2, 3)] if t == 0 else [])
+        K = T.kb[:, 0:104]
+        kx = P([mm(K, A0("w7"), A0("cj"), True, False)], 104, ["w7", "cj"] + YK("y2", h), ["K" + hs], acq="kb")
+        P([mm(K, ta(a), A0("RT"), False, False) for a in range(4)], 416, TK + ["RT"], [], acc="K" + hs, use=kx)
+        P([mm(K, H("y2", h, m, None, 16), T.Z[:, :, 19 - m:32 - m], False, False) for m in range(16)], 1664,
+          YK("y2", h) + ["Z"], [], acc="K" + hs, use=kx)
+        yx = P([mm(T.yps[:, 32 * b:32 * b + 32, :], A0("Ib"), H("y2", h, 512 * b, 512 * b + 512)) for b in range(4)], 2048,
+               YK("y2", h) + ["Ib"], ["yps" + hs], acq="yps")
+        ja, jv = list(range(J0, J)), list(range(J0))
+        for x, j in enumerate(ja):
+            dx = P([mm(T.dif[:, 128 * a:128 * a + 128], A0("Ib"), H("y2", h, j + a, None, 16), True, False) if w == 0 else
+                    mm(T.dif[:, 128 * a:128 * a + 128], A0("Im"), ta(a), False, True) for a in range(4) for w in range(2)], 1024,
+                   YK("y2", h) + TK + ["Ib", "Im"], ["dif" + hs], acq="dif")
+            b = x
+            A(act(H("Ma", h, 512 * b, 512 * b + 512), T.dif[:, :], AF.Relu), 512, ["dif" + hs], ["Ma%s%d" % (hs, b)], use=dx)
+            P([mm(T.kb[:, j:104:13], H("Ma", h, 512 * b + 128 * a, 512 * b + 128 * a + 128), A0("G32"), False, False) for a in range(4)],
+              256, ["Ma%s%d" % (hs, b), "G32"], [], acc="K" + hs, use=kx)
+        for j in jv:
+            n = mcount[0] % NM
+            mcount[0] += 1
+            M = T["mb%d" % n]
+            V(tt(M[:, :, :], T.yps[:, :, j:j + 4], tl, Op.max), 512, ["yps" + hs] + TK, ["mb%d" % n], use=yx)
+            P([mm(T.kb[:, j:104:13], M[:, :, a], A0("G32"), False, False) for a in range(4)], 256, ["mb%d" % n, "G32"], [], acc="K" + hs, use=kx)
+        V(scan(H("ks", h), A0("KD"), K, Op.max, Op.min), 104, ["K" + hs, "KD"], ["ks" + hs], use=kx)
+
+    def decide(t, h):
+        hs = str(h)
+        best = H("ks", h, 12, None, 13)
+        tie, dlt = H("Xs", h, 0, 128, 16), H("Xs", h, 128, 256, 16)
+        V(ts(H("rr", h), best, MAGIC, MAGIC, Op.add, Op.subtract), 8, ["ks" + hs], ["rr" + hs])
+        V(ts(tie, best, EARLY, None, Op.is_lt), 8, ["ks" + hs, "Xs" + hs], ["Xs" + hs])
+        V(tt(H("dd", h), H("rr", h), best, Op.subtract), 16, ["rr" + hs, "ks" + hs], ["dd" + hs])
+        V(tt(dlt, H("dd", h), tie, Op.mult), 16, ["dd" + hs, "Xs" + hs], ["Xs" + hs])
+        V(scan(H("Xr", h), A0("RD"), H("Xs", h), Op.mult, Op.add), 128, ["RD", "RD2", "Xs" + hs], ["Xr" + hs])
+
+    def fresh(t, h):
+        hs, c0 = str(h), 128 * h
+        X = T.vt[:, 256 * h:256 * h + 128]
+        Y = T.vt[:, 256 * h + 128:256 * h + 256]
+        dn, sn = "dg%d" % (t % 2), "st%d" % ((t + 1) % 2)
+        tx = P([mm(T.sm[:, 0:128], A0("w7"), A0("cm16"), True, False), mm(T.sm[:, 0:128], H("Xr", h, 0, 128), A0("I16"), False, True),
+                mm(T.sm[:, 128:256], H("Xr", h, 128, 256), A0("Ib"))], 384, ["w7", "cm16", "I16", "Ib", "Xr" + hs], ["tz" + hs], acq="sm")
+        V(tt(Y, zref(t, h), T.sm[:, 0:128], Op.add), 128, ["z%d%d" % (t, h), "tz" + hs], ["vY" + hs], use=tx)
+        V(tt(H("dge", h), T.sm[:, 128:256], H("geb", h), Op.mult), 128, ["tz" + hs, "geb" + hs], ["dge" + hs], use=tx)
+        V(ts(H("zp", h), Y, 0.0, None, Op.max), 128, ["vY" + hs], ["zp" + hs])
+        V(tt(X, H("zp", h), T.sg[:, c0:c0 + 128], Op.subtract), 256, ["zp" + hs, "sg"], ["vX" + hs])
+        V(ts(H("cmp", h), X, 0.0, None, Op.is_ge), 128, ["vX" + hs], ["cmp" + hs])
+        V(tt(Y, X, H("dge", h), Op.subtract), 128, ["vX" + hs, "dge" + hs], ["vY" + hs])
+        V(tt(H("Hb", h), Y, T[dn][:, c0:c0 + 128], Op.mult), 128, ["vY" + hs, dn], ["Hb" + hs])
+        V(tt(T[sn][:, c0:c0 + 128], H("dge", h), T.sg[:, c0:c0 + 128], Op.add), 256, ["dge" + hs, "sg"], ["%s_%d" % (sn, h)])
+        select(t, h, "W1", 1)
+        samples(h, "v2")
+
+    def counts(t):
+        tx = P([mm(T.sm[:, 0:1], H("Xr", 0, 0, 128), T.c205[:, 0:1], True, False), mm(T.sm[:, 0:1], H("Xr", 1, 0, 128), T.c205[:, 0:1], False, True)],
+               128, ["Xr0", "Xr1", "c205"], ["Aps"], acq="sm")
+        V(cp(T.am[:, 4 * t:4 * t + 1], T.sm[:, 0:1]), 1, ["Aps"], ["am%d" % t], use=tx)
+        send(t, "A", None, T.al[:, 4 * t + 4:4 * t + 5], T.am[:, 4 * t:4 * t + 1], "am%d" % t)
+
+    def send(t, kind, h, out, in_, key):
+        sem = "r%s%d%s" % (kind, t + 1, "" if h is None else h)
+        rid, pid, mask = nxt
+
+        def fn(last):
+            return g.remote_dma(out, in_, T.sem[sem], T.sem.loc, pid, rid, mask)
+        i = add("q", [fn], 0.9, [key], [], pin=("send",))
+        add("n", [], 3.0, [], ["%s%d%s" % (kind, t + 1, "" if h is None else h)], after=[i], pin=(sem, gs["neng"]))
+
+    def finish(t, h):
+        hs = str(h)
+        for q in range(3):
+            fns = []
+            for w in range(4):
+                m = 4 + 4 * q + w
+                fns += [mm(T.dif[:, 128 * w:128 * w + 128], A0("Ib"), H("v2", h, m, None, 16), True, False),
+                        mm(T.dif[:, 128 * w:128 * w + 128], A0("Im"), H("v2", h, m - 1, None, 16), False, True)]
+            dx = P(fns, 1024, YK("v2", h) + ["Ib", "Im"], ["dif" + hs], acq="dif")
+            A(act(H("Va", h, 512 * q, 512 * q + 512), T.dif[:, :], AF.Abs), 512, ["dif" + hs], ["Va%s%d" % (hs, q)], use=dx)
+        fns = [mm(T.sm[:, 0:104], A0("w7"), A0("cpad"), True, False)]
+        for w in range(12):
+            fns.append(mm(T.sm[:, 12 - w:104:13], H("Va", h, 128 * w, 128 * w + 128), A0("G1"), False, w == 11))
+        tx = P(fns, 104 + 768, ["w7", "cpad", "G1"] + ["Va%s%d" % (hs, q) for q in range(3)], ["S" + hs], acq="sm")
+        V(ts(H("nx", h), T.sm[:, 0:104], 820.0, None, Op.is_le), 104, ["S" + hs], ["nx" + hs], use=tx)
+        V(scan(H("ns", h), A0("ONE"), H("nx", h), Op.add, Op.mult), 104, ["ONE", "nx" + hs], ["ns" + hs])
+        V(cp(H("Xn", h, 0, 128, 16), H("ns", h, 12, None, 13)), 8, ["ns" + hs, "Xn" + hs], ["Xn" + hs])
+        V(scan(H("Xnr", h), T.RD[:, 0:128], H("Xn", h), Op.mult, Op.add), 64, ["RD", "Xn" + hs], ["Xnr" + hs])
+        tx = P([mm(T.sm[:, 0:128], A0("w7"), A0("c3"), True, False), mm(T.sm[:, 0:128], H("Xnr", h), A0("Ib"), False, True)], 256,
+               ["w7", "c3", "Xnr" + hs, "Ib"], ["n" + hs], acq="sm")
+        a = A(act(H("nsb", h), T.sm[:, 0:128]), 128, ["n" + hs], ["nsb" + hs], use=tx)
+        zo = T.zm[:, 256 * t + 128 * h:256 * t + 128 * h + 128]
+        V(tt(zo, H("zp", h), T.sm[:, 0:128], Op.add), 128, ["zp" + hs, "n" + hs], ["zm%d%d" % (t, h)], use=tx, after=[a])
+        send(t, "z", h, T.zl[:, 256 * t + 128 * h:256 * t + 128 * h + 128], zo, "zm%d%d" % (t, h))
+        tx = P([mm(T.sm[:, 0:32], A0("Ih"), A0("Qc"), True, False)] +
+               [mm(T.sm[:, 0:32], T.Wu[:, 128 * u:128 * u + 128], H("nsb", h, u, None, 4), False, u == 3) for u in range(4)], 320,
+               ["Ih", "Qc", "nsb" + hs] + ["Wu%d" % u for u in range(4)], ["Q" + hs], acq="sm")
+        V(cp(H("tof", h), T.sm[:, 0:32]), 32, ["Q" + hs], ["tof" + hs], use=tx)
+        to = T.ts[:, 1024 * t + 512 * h:1024 * t + 512 * h + 512]
+        A(act(to, H("v2", h).indirect(H("tof", h))), 512 * 1.5, YK("v2", h) + ["tof" + hs], ["ts%d%d" % (t, h)])
+        send(t, "T", h, T["tl%d" % (t + 1)][:, 128 * h:128 * h + 128, :], to, "ts%d%d" % (t, h))
+
+    for t in range(NV):
+        gatherlist(t)
+        for h in range(2):
+            front(t, h)
+        for h in range(2):
+            heavy(t, h)
+            decide(t, h)
+            fresh(t, h)
+        if t < NV - 1:
+            counts(t)
+        for h in range(2):
+            finish(t, h)
+
+    st = "st%d" % (NV % 2)
+    V(ts(A0("li"), A0("LF"), T.al[:, 4 * NV - 4:4 * NV - 3], None, Op.subtract), 16, ["LF", "A%d" % (NV - 1)], ["li"])
+    C(ts(A0("lm"), A0("li"), 255, None, Op.bitwise_and), 16, ["li"], "lm")
+    C(cp(A0("lu"), A0("lm")), 16, ["lm"], "lu")
+    A(act(A0("ysb"), T[st][:, :].indirect(T.lu[:, :])), 256 * 1.5, ["lu", st + "_0", st + "_1"], ["ysb"])
+
+    def store(out, in_, rd):
+        add("d", [lambda last: gs["d"].dma_start(out, in_)], 2.0, rd, [], pin=("sto", 16))
+    store(T.ys[:, :], T.ysb[:, :], ["ysb"])
+    for h in range(2):
+        c = 256 * (NV - 1) + 128 * h
+        store(T.yz[:, 128 * h:128 * h + 128], T.zl[0:128:16, c:c + 128], ["z%d%d" % (NV, h)])
+    fin = []
+    for h in range(2):
+        for a in range(4):
+            src = T["tl%d" % NV][:, 128 * h:128 * h + 128, a]
+            dst = T.ytb[:, 256 * a + 128 * h:256 * a + 128 * h + 128]
+            key = "yt%d%d" % (h, a)
+            fin.append(key)
+            if a < 2:
+                V(cp(dst, src), 64, ["T%d%d" % (NV, h)], [key])
+            else:
+                A(act(dst, src), 128, ["T%d%d" % (NV, h)], [key])
+    store(T.yt[:, :], T.ytb[:, :], fin)
+    return ops
+
+
+def schedule(ops):
+    n = len(ops)
+    succ = [[] for _ in range(n)]
+    for i, o in enumerate(ops):
+        for d in o["deps"]:
+            succ[d].append(i)
+    pr = [0.0] * n
+    for i in range(n - 1, -1, -1):
+        pr[i] = ops[i]["cost"] + 0.04 + max([pr[k] for k in succ[i]], default=0.0)
+    left = [len(o["deps"]) for o in ops]
+    members = {}
+    for i, o in enumerate(ops):
+        if o["use"] is not None:
+            members.setdefault(o["use"], []).append(i)
+    ready = {e: [] for e in "vapqdn"}
+    for i in range(n):
+        if left[i] == 0:
+            ready[ops[i]["eng"]].append(i)
+    free = {e: 0.0 for e in "vapqdn"}
+    end, order, holder, pend = [0.0] * n, [], {}, {}
+    dep_end = [0.0] * n
+    while len(order) < n:
+        best = None
+        for e in "vapqdn":
+            cand = []
+            for i in ready[e]:
+                o = ops[i]
+                b = o["acq"]
+                est = dep_end[i]
+                if b is not None and b in holder:
+                    tx = holder[b]
+                    if pend[tx] > 0:
+                        continue
+                    est = max(est, max(end[m] for m in members[tx]) + 0.04)
+                if e in "vapq":
+                    est = max(est, free[e])
+                cand.append((est, i))
+            if not cand:
+                continue
+            lo = min(c[0] for c in cand) + 0.05
+            est, i = max((c for c in cand if c[0] <= lo), key=lambda c: pr[c[1]])
+            if best is None or est < best[0]:
+                best = (est, i, e)
+        est, i, e = best
+        o = ops[i]
+        ready[e].remove(i)
+        if o["acq"] is not None:
+            b = o["acq"]
+            if b in holder:
+                for m in members[holder[b]]:
+                    o["deps"].setdefault(m, False)
+            holder[b] = i
+            pend[i] = len(members[i])
+        if o["use"] is not None:
+            pend[o["use"]] -= 1
+        end[i] = est + o["cost"]
+        if e in "vapq":
+            free[e] = end[i]
+        order.append((est, i))
+        for k in succ[i]:
+            left[k] -= 1
+            dep_end[k] = max(dep_end[k], end[i] + 0.04)
+            if left[k] == 0:
+                ready[ops[k]["eng"]].append(k)
+    return [i for _, i in order], end
+
+
+def emit(ops, order, T, gs):
+    lastacc = {}
+    for i in order:
+        if ops[i]["eng"] == "p" and ops[i]["use"] is not None:
+            lastacc[ops[i]["use"]] = i
+    count = {}
+    done = {}
+    know = {e: {} for e in "vapqd"}
+
+    def after(e, i, raw):
+        o = ops[i]
+        sem, val, clk = done[i]
+        if o["eng"] == e and not raw:
+            return
+        if know[e].get(sem, 0) >= val:
+            return
+        gs[e].wait_ge(T.sem[sem], val)
+        for k, w in clk.items():
+            if know[e].get(k, 0) < w:
+                know[e][k] = w
+        know[e][sem] = max(val, know[e].get(sem, 0))
+    for i in order:
+        o = ops[i]
+        e = o["eng"]
+        if e == "n":
+            done[i] = (o["sym"][0], o["sym"][1], {})
+            continue
+        ds = sorted(o["deps"].items(), key=lambda d: -done[d[0]][1] if d[0] in done else 0)
+        for d, raw in ds:
+            after(e, d, raw)
+        for x, fn in enumerate(o["fns"]):
+            last = e == "p" and lastacc.get(o["use"]) == i and x == len(o["fns"]) - 1
+            c = fn(last)
+            if e in "vap" or (e == "q" and o["sym"] is None):
+                c.then_inc(T.sem[e], 1)
+                count[e] = count.get(e, 0) + 1
+            elif e == "d":
+                sem, add = o["sym"]
+                c.then_inc(T.sem[sem], add)
+                count[sem] = count.get(sem, 0) + add
+            else:
+                count["loc"] = count.get("loc", 0) + gs["neng"]
+        sem = e if e in "vap" or (e == "q" and o["sym"] is None) else ("loc" if e == "q" else o["sym"][0])
+        done[i] = (sem, count[sem], dict(know[e]))
+    gs["d"].wait_ge(T.sem.sto, count["sto"])
+    for sem in ("v", "a", "p", "q", "loc"):
+        gs["q"].wait_ge(T.sem[sem], count[sem])
+
+
+def rank_program(g, core, T, topo):
+    rank = T.rank_of(core)
+    if rank is None:
+        return
+    dst = T.cores[(rank + 1) % len(T.cores)]
+    rid, pid, _ = topo.addr(dst)
+    gs = {"v": g.vector, "a": g.scalar, "p": g.tensor, "q": g, "d": g.sync, "neng": len(topo.engines(core, dst))}
+    ops = build(T, gs, (rid, pid, topo.mask(core, dst)))
+    order, _ = schedule(ops)
+    emit(ops, order, T, gs)

@@ -3,9 +3,15 @@ from concourse.mybir import dt, AluOpType as Op, ActivationFunctionType as AF
 
 NV = 8
 J = 13
-J0 = 9
+JA = (11, 9)
 NM = 4
-GP = 2
+GP = 4
+EY = (0, 1)
+ZP = (0,)
+VG = (("v2", 1, 1), ("y2", 0, 1), ("y2", 0, 3), ("v2", 1, 3))
+WIN = 0.02
+BONUS = {("F", 0): -96.8, ("H", 0): -145.4, ("D", 0): 78.0, ("N", 0): 229.2, ("E", 0): -208.8, ("L", 0): 199.4, ("C", 0): -76.6,
+         ("F", 1): -136.4, ("H", 1): -204.6, ("D", 1): -162.2, ("N", 1): 211.4, ("E", 1): -111.2}
 MAGIC = 201326592.0
 EARLY, LATE = 37528.0, 1.0e9
 
@@ -24,11 +30,11 @@ SCRATCH = {
     "sh": ("sbuf", [128, 32], I32), "q1": ("sbuf", [128, 32], I32), "q2": ("sbuf", [128, 32], I32), "l5": ("sbuf", [128, 16], I32),
     "w9": ("sbuf", [128, 128], F32), "w18": ("sbuf", [128, 128], F32), "mu": ("sbuf", [128, 32], F32), "shf": ("sbuf", [128, 8], F32),
     "gf": ("sbuf", [128, 8], F32), "gr": ("sbuf", [128, 104], F32), "sg1": ("sbuf", [128, 104], F32), "sg2": ("sbuf", [128, 104], F32),
-    "B32": ("sbuf", [128, 128], F32), "Bb": ("sbuf", [128, 128], BF), "Ib": ("sbuf", [128, 128], BF), "I16": ("sbuf", [128, 128], BF),
+    "B32": ("sbuf", [128, 128], F32), "I32": ("sbuf", [128, 128], F32), "Bb": ("sbuf", [128, 128], BF), "Ib": ("sbuf", [128, 128], BF), "I16": ("sbuf", [128, 128], BF),
     "Im": ("sbuf", [128, 128], BF), "Ih": ("sbuf", [128, 128], F16), "W0": ("sbuf", [128, 128], F16), "W1": ("sbuf", [128, 128], F16),
     "Wu": ("sbuf", [128, 512], BF), "G1": ("sbuf", [128, 8], BF), "G32": ("sbuf", [128, 8], BF), "Z": ("sbuf", [128, 8, 32], BF),
-    "RT": ("sbuf", [128, 104], BF), "cj": ("sbuf", [128, 104], BF), "cpad": ("sbuf", [128, 104], BF), "KD": ("sbuf", [128, 104], F32),
-    "ONE": ("sbuf", [128, 104], F32), "RD": ("sbuf", [128, 256], BF), "Qc": ("sbuf", [128, 32], F16), "rp1": ("sbuf", [128, 8], F32),
+    "RT0": ("sbuf", [128, 104], BF), "RT1": ("sbuf", [128, 104], BF), "cj": ("sbuf", [128, 104], BF), "cpad": ("sbuf", [128, 104], BF), "KD": ("sbuf", [128, 104], F32),
+    "ONE": ("sbuf", [128, 104], F32), "RD": ("sbuf", [128, 128], BF), "Qc": ("sbuf", [128, 32], F16), "rp1": ("sbuf", [128, 8], F32),
     "LB": ("sbuf", [128, 16], F32), "LF": ("sbuf", [128, 16], F32), "R8": ("sbuf", [8, 128], F32),
     "w7": ("sbuf", [128, 128], BF), "c185": ("sbuf", [128, 128], BF), "cm16": ("sbuf", [128, 128], BF), "c3": ("sbuf", [128, 128], BF),
     "c205": ("sbuf", [128, 8], BF),
@@ -36,13 +42,14 @@ SCRATCH = {
     "kb": ("psum", [128, 512], F32), "sm": ("psum", [128, 512], F32),
 }
 _HALF = {"cmp": (128, BF), "geb": (128, BF), "Hb": (128, F32), "oH": (128, F32), "oD": (128, F16), "fi": (128, I32), "fm": (128, I32),
-         "of": (128, U16), "y2": (2048, BF), "v2": (2048, BF), "Va": (1536, BF), "ks": (104, F32), "rr": (8, F32), "dd": (8, F32),
+         "of": (128, U16), "y2": (2048, BF), "v2": (2064, BF), "Va": (1536, BF), "ks": (104, F32), "rr": (8, F32), "dd": (8, F32),
          "Xs": (256, BF), "Xr": (256, BF), "dge": (128, F32), "zp": (128, F32), "nx": (104, F32), "ns": (104, F32), "Xn": (128, BF),
-         "Xnr": (128, BF), "nsb": (128, BF), "tof": (32, U16), "Ma": (512 * (J - J0), BF)}
+         "Xnr": (128, BF), "nsb": (128, BF), "tof": (32, U16), "Ma": (512 * (J - min(JA)), BF)}
 for _n, (_c, _d) in _HALF.items():
     SCRATCH[_n] = ("sbuf", [128, 2 * _c], _d)
 for _m in range(NM):
     SCRATCH["mb%d" % _m] = ("sbuf", [128, 128, 4], BF)
+SCRATCH["Vb"] = ("sbuf", [128, 256, 12], BF)
 SCRATCH["ts"] = ("sbuf", [128, NV * 1024], BF)
 for _t in range(NV + 1):
     SCRATCH["tl%d" % _t] = ("sbuf", [128, 256, 4], BF)
@@ -53,7 +60,7 @@ SEMAPHORES.remove("rA%d" % NV)
 
 
 def build(T, gs, nxt):
-    ops, lastw, readers, accs = [], {}, {}, {}
+    ops, lastw, readers, accs, tag = [], {}, {}, {}, [("I", 0)]
 
     def add(eng, fns, cost, rd=(), wr=(), acc=None, acq=None, use=None, after=(), pin=None):
         i = len(ops)
@@ -74,7 +81,7 @@ def build(T, gs, nxt):
             deps[o] = deps.get(o, False)
         if acq is not None:
             use = i
-        ops.append(dict(eng=eng, fns=fns, cost=cost, deps=deps, acq=acq, use=use, sym=pin))
+        ops.append(dict(eng=eng, fns=fns, cost=cost, deps=deps, acq=acq, use=use, sym=pin, tag=tag[0], wr=tuple(wr)))
         return i
 
     v, s, p, g = gs["v"], gs["a"], gs["p"], gs["q"]
@@ -148,6 +155,7 @@ def build(T, gs, nxt):
     C(tt(T.R8[:, :], T.iP[0:8, :], T.qg[0:8, :], Op.is_equal), 256, ["iP", "qg"], "R8")
     A(act(A0("Bb"), A0("B32")), 128, ["B32"], ["Bb"])
     C(tt(A0("Ib"), A0("iP"), A0("iQ"), Op.is_equal), 256, ["iP", "iQ"], "Ib")
+    A(act(A0("I32"), A0("Ib")), 128, ["Ib"], ["I32"])
     A(act(A0("I16"), A0("Ib"), scale=16.0), 128, ["Ib"], ["I16"])
     A(act(A0("Im"), A0("Ib"), scale=-1.0), 128, ["Ib"], ["Im"])
     C(cp(A0("Ih"), A0("Ib")), 64, ["Ib"], "Ih")
@@ -165,11 +173,12 @@ def build(T, gs, nxt):
     C(ts(A0("cpad"), A0("iJ"), 0.0, 1000.0, Op.is_equal, Op.mult), 104, ["iJ"], "cpad")
     C(ts(A0("KD"), A0("iJ"), 0.0, LATE, Op.is_equal, Op.mult), 104, ["iJ"], "KD")
     C(tt(A0("gr"), T.pg[:, 0:104], A0("iC"), Op.is_equal), 208, ["pg", "iC"], "gr")
-    C(ts(A0("sg1"), A0("iJ"), float(J0), 32.0, Op.is_ge, Op.mult), 104, ["iJ"], "sg1")
-    C(ts(A0("sg2"), A0("sg1"), -16.0, None, Op.add), 104, ["sg1"], "sg2")
-    C(tt(A0("RT"), A0("sg2"), A0("gr"), Op.mult), 208, ["sg2", "gr"], "RT")
+    for h in range(2 if JA[0] != JA[1] else 1):
+        C(ts(A0("sg1"), A0("iJ"), float(JA[h]), 32.0, Op.is_ge, Op.mult), 104, ["iJ"], "sg1")
+        C(ts(A0("sg2"), A0("sg1"), -16.0, None, Op.add), 104, ["sg1"], "sg2")
+        C(tt(A0("RT%d" % h), A0("sg2"), A0("gr"), Op.mult), 208, ["sg2", "gr"], "RT%d" % h)
+    RT = ["RT0", "RT%d" % (JA[0] != JA[1])]
     C(ts(T.RD[:, 0:128], A0("qm"), 0.0, None, Op.is_gt), 128, ["qm"], "RD")
-    C(ts(T.RD[:, 128:256], A0("qm"), 0.0, None, Op.is_gt), 128, ["qm"], "RD2")
     C(ts(A0("sh"), T.pm[:, 0:32], 2, None, Op.arith_shift_right), 32, ["pm"], "sh")
     C(ts(A0("q1"), A0("sh"), 12.0, None, Op.mult), 32, ["sh"], "q1")
     C(tt(A0("q2"), A0("q1"), T.pm[:, 0:32], Op.add), 64, ["q1", "pm"], "q2")
@@ -183,6 +192,8 @@ def build(T, gs, nxt):
     fill("c3", 3.0, 64)
     fill("c205", 205.0, 8)
     fill("ONE", 1.0, 104)
+    for h in EY:
+        C((lambda h: lambda last: v.memset(H("v2", h, 2048, 2064), 0.0))(h), 16, [], "v2p%d" % h)
     for h in range(2):
         C((lambda h: lambda last: v.memset(H("Xs", h), 0.0))(h), 128, [], "Xs%d" % h)
         C((lambda h: lambda last: v.memset(H("Xn", h), 0.0))(h), 64, [], "Xn%d" % h)
@@ -236,8 +247,9 @@ def build(T, gs, nxt):
             V(ts(H("geb", h), T.sm[:, 0:128], T.rp1[:, 0:1], None, Op.is_le), 128, ["cnt" + hs, "rp1"], ["geb" + hs], use=tx)
         V(tt(H("oD", h), OHS, T[dn][:, c0:c0 + 128], Op.mult), 128, [OK + hs, dn], ["oD" + hs])
         V(tt(H("oH", h), OHS, H("Hb", h), Op.mult), 128, [OK + hs, "Hb" + hs], ["oH" + hs])
-        tx = P([mm(T.sm[:, 0:128], A0("w7"), A0("c185"), True, False), mm(T.sm[:, 0:128], A0(W), H("oD", h), False, False),
-                mm(T.sm[:, 0:128], A0("B32"), H("oH", h), False, True)], 768, ["w7", "c185", W, "oD" + hs, "oH" + hs, "B32"], ["F" + hs], acq="sm")
+        tx = P([mm(T.sm[:, 0:128], A0("w7"), A0("c185"), True, False), mm(T.sm[:, 0:128], A0(W), H("oD", h), False, False)], 256,
+               ["w7", "c185", W, "oD" + hs], ["F" + hs], acq="sm")
+        P([mm(T.sm[:, 0:128], A0("B32"), H("oH", h), False, True)], 512, ["oH" + hs, "B32"], ["F" + hs], use=tx)
         V(cp(H("fi", h), T.sm[:, 0:128]), 128, ["F" + hs], ["fi" + hs], use=tx)
         V(ts(H("fm", h), H("fi", h), 4095, None, Op.bitwise_and), 128, ["fi" + hs], ["fm" + hs])
         V(cp(H("of", h), H("fm", h)), 128, ["fm" + hs], ["of" + hs])
@@ -245,8 +257,9 @@ def build(T, gs, nxt):
     def samples(h, buf):
         hs, k = str(h), 128 // GP
         for q in range(GP):
-            A(act(H(buf, h, 16 * k * q, 16 * k * q + 16 * k), T.x[:, :].indirect(H("of", h, k * q, k * q + k))), 16 * k * 1.5,
-              ["x", "of" + hs], [buf + hs + "_%d" % q])
+            on_v = (buf, h, q) in VG
+            (V if on_v else A)((cp if on_v else act)(H(buf, h, 16 * k * q, 16 * k * q + 16 * k), T.x[:, :].indirect(H("of", h, k * q, k * q + k))),
+                               16 * k * 1.5, ["x", "of" + hs], [buf + hs + "_%d" % q])
     YK = lambda b, h: [b + str(h) + "_%d" % q for q in range(GP)]
 
     def front(t, h):
@@ -266,12 +279,15 @@ def build(T, gs, nxt):
         TK = ["T%d%d" % (t, h)] + (["T0%d_%d" % (h, a) for a in (1, 2, 3)] if t == 0 else [])
         K = T.kb[:, 0:104]
         kx = P([mm(K, A0("w7"), A0("cj"), True, False)], 104, ["w7", "cj"] + YK("y2", h), ["K" + hs], acq="kb")
-        P([mm(K, ta(a), A0("RT"), False, False) for a in range(4)], 416, TK + ["RT"], [], acc="K" + hs, use=kx)
+        P([mm(K, ta(a), A0(RT[h]), False, False) for a in range(4)], 416, TK + [RT[h]], [], acc="K" + hs, use=kx)
         P([mm(K, H("y2", h, m, None, 16), T.Z[:, :, 19 - m:32 - m], False, False) for m in range(16)], 1664,
           YK("y2", h) + ["Z"], [], acc="K" + hs, use=kx)
-        yx = P([mm(T.yps[:, 32 * b:32 * b + 32, :], A0("Ib"), H("y2", h, 512 * b, 512 * b + 512)) for b in range(4)], 2048,
-               YK("y2", h) + ["Ib"], ["yps" + hs], acq="yps")
-        ja, jv = list(range(J0, J)), list(range(J0))
+        yx = None
+        for b in range(4):
+            fill_b = [mm(T.yps[:, 32 * b:32 * b + 32, :], A0("Ib"), H("y2", h, 512 * b, 512 * b + 512))]
+            y = P(fill_b, 512, ["y2%s_%d" % (hs, b * GP // 4), "Ib"], ["yps%s%d" % (hs, b)], **({"acq": "yps"} if b == 0 else {"use": yx, "after": [yx]}))
+            yx = y if b == 0 else yx
+        ja, jv = list(range(JA[h], J)), list(range(JA[h]))
         for x, j in enumerate(ja):
             dx = P([mm(T.dif[:, 128 * a:128 * a + 128], A0("Ib"), H("y2", h, j + a, None, 16), True, False) if w == 0 else
                     mm(T.dif[:, 128 * a:128 * a + 128], A0("Im"), ta(a), False, True) for a in range(4) for w in range(2)], 1024,
@@ -284,7 +300,7 @@ def build(T, gs, nxt):
             n = mcount[0] % NM
             mcount[0] += 1
             M = T["mb%d" % n]
-            V(tt(M[:, :, :], T.yps[:, :, j:j + 4], tl, Op.max), 512, ["yps" + hs] + TK, ["mb%d" % n], use=yx)
+            V(tt(M[:, :, :], T.yps[:, :, j:j + 4], tl, Op.max), 512, ["yps%s%d" % (hs, b) for b in range(4)] + TK, ["mb%d" % n], use=yx)
             P([mm(T.kb[:, j:104:13], M[:, :, a], A0("G32"), False, False) for a in range(4)], 256, ["mb%d" % n, "G32"], [], acc="K" + hs, use=kx)
         V(scan(H("ks", h), A0("KD"), K, Op.max, Op.min), 104, ["K" + hs, "KD"], ["ks" + hs], use=kx)
 
@@ -292,22 +308,31 @@ def build(T, gs, nxt):
         hs = str(h)
         best = H("ks", h, 12, None, 13)
         tie, dlt = H("Xs", h, 0, 128, 16), H("Xs", h, 128, 256, 16)
+        V(ts(tie, best, EARLY, None, Op.is_lt), 8, ["ks" + hs, "Xs" + hs], ["Xt" + hs])
+        V(scan(H("Xr", h, 0, 128), T.RD[:, 0:128], H("Xs", h, 0, 128), Op.mult, Op.add), 64, ["RD", "Xt" + hs], ["Xr" + hs])
         V(ts(H("rr", h), best, MAGIC, MAGIC, Op.add, Op.subtract), 8, ["ks" + hs], ["rr" + hs])
-        V(ts(tie, best, EARLY, None, Op.is_lt), 8, ["ks" + hs, "Xs" + hs], ["Xs" + hs])
         V(tt(H("dd", h), H("rr", h), best, Op.subtract), 16, ["rr" + hs, "ks" + hs], ["dd" + hs])
-        V(tt(dlt, H("dd", h), tie, Op.mult), 16, ["dd" + hs, "Xs" + hs], ["Xs" + hs])
-        V(scan(H("Xr", h), A0("RD"), H("Xs", h), Op.mult, Op.add), 128, ["RD", "RD2", "Xs" + hs], ["Xr" + hs])
+        V(tt(dlt, H("dd", h), tie, Op.mult), 16, ["dd" + hs, "Xt" + hs], ["Xd" + hs])
+        V(scan(H("Xr", h, 128, 256), T.RD[:, 0:128], H("Xs", h, 128, 256), Op.mult, Op.add), 64, ["RD", "Xd" + hs], ["Xe" + hs])
 
     def fresh(t, h):
         hs, c0 = str(h), 128 * h
         X = T.vt[:, 256 * h:256 * h + 128]
         Y = T.vt[:, 256 * h + 128:256 * h + 256]
         dn, sn = "dg%d" % (t % 2), "st%d" % ((t + 1) % 2)
-        tx = P([mm(T.sm[:, 0:128], A0("w7"), A0("cm16"), True, False), mm(T.sm[:, 0:128], H("Xr", h, 0, 128), A0("I16"), False, True),
-                mm(T.sm[:, 128:256], H("Xr", h, 128, 256), A0("Ib"))], 384, ["w7", "cm16", "I16", "Ib", "Xr" + hs], ["tz" + hs], acq="sm")
-        V(tt(Y, zref(t, h), T.sm[:, 0:128], Op.add), 128, ["z%d%d" % (t, h), "tz" + hs], ["vY" + hs], use=tx)
-        V(tt(H("dge", h), T.sm[:, 128:256], H("geb", h), Op.mult), 128, ["tz" + hs, "geb" + hs], ["dge" + hs], use=tx)
-        V(ts(H("zp", h), Y, 0.0, None, Op.max), 128, ["vY" + hs], ["zp" + hs])
+        zk = "z%d%d" % (t, h)
+        if h in ZP:
+            tx = P([mm(T.sm[:, 0:128], A0("w7"), A0("cm16"), True, False), mm(T.sm[:, 0:128], A0("I32"), zref(t, h), False, False),
+                    mm(T.sm[:, 0:128], H("Xr", h, 0, 128), A0("I16"), False, True)], 768, ["w7", "cm16", "I16", "I32", "Xr" + hs, zk], ["tz" + hs], acq="sm")
+            A(act(H("zp", h), T.sm[:, 0:128], AF.Relu), 128, ["tz" + hs], ["zp" + hs], use=tx)
+            tx = P([mm(T.sm[:, 128:256], H("Xr", h, 128, 256), A0("Ib"))], 128, ["Ib", "Xe" + hs], ["td" + hs], acq="sm")
+            V(tt(H("dge", h), T.sm[:, 128:256], H("geb", h), Op.mult), 128, ["td" + hs, "geb" + hs], ["dge" + hs], use=tx)
+        else:
+            tx = P([mm(T.sm[:, 0:128], A0("w7"), A0("cm16"), True, False), mm(T.sm[:, 0:128], H("Xr", h, 0, 128), A0("I16"), False, True),
+                    mm(T.sm[:, 128:256], H("Xr", h, 128, 256), A0("Ib"))], 384, ["w7", "cm16", "I16", "Ib", "Xr" + hs, "Xe" + hs], ["tz" + hs], acq="sm")
+            V(tt(Y, zref(t, h), T.sm[:, 0:128], Op.add), 128, [zk, "tz" + hs], ["vY" + hs], use=tx)
+            V(tt(H("dge", h), T.sm[:, 128:256], H("geb", h), Op.mult), 128, ["tz" + hs, "geb" + hs], ["dge" + hs], use=tx)
+            V(ts(H("zp", h), Y, 0.0, None, Op.max), 128, ["vY" + hs], ["zp" + hs])
         V(tt(X, H("zp", h), T.sg[:, c0:c0 + 128], Op.subtract), 256, ["zp" + hs, "sg"], ["vX" + hs])
         V(ts(H("cmp", h), X, 0.0, None, Op.is_ge), 128, ["vX" + hs], ["cmp" + hs])
         V(tt(Y, X, H("dge", h), Op.subtract), 128, ["vX" + hs, "dge" + hs], ["vY" + hs])
@@ -333,7 +358,16 @@ def build(T, gs, nxt):
 
     def finish(t, h):
         hs = str(h)
-        for q in range(3):
+        ex = None
+        for b in range(4 if h in EY else 0):
+            e = P([mm(T.yps[:, 32 * b:32 * b + 32, :], A0("Ib"), H("v2", h, 512 * b + 1, 512 * b + 513), True, False),
+                   mm(T.yps[:, 32 * b:32 * b + 32, :], A0("Im"), H("v2", h, 512 * b, 512 * b + 512), False, True)], 1024,
+                  ["v2%s_%d" % (hs, k) for k in sorted({b * GP // 4, min(b + 1, 3) * GP // 4})] + ["v2p" + hs, "Ib", "Im"], ["yps%s%d" % (hs, b)],
+                  **({"acq": "yps"} if b == 0 else {"use": ex, "after": [ex]}))
+            ex = e if b == 0 else ex
+            A(act(T.Vb[:, 128 * h + 32 * b:128 * h + 32 * b + 32, :], T.yps[:, 32 * b:32 * b + 32, 3:15], AF.Abs), 384,
+              ["yps%s%d" % (hs, b)], ["Vb%s%d" % (hs, b)], use=ex)
+        for q in range(0 if h in EY else 3):
             fns = []
             for w in range(4):
                 m = 4 + 4 * q + w
@@ -343,8 +377,10 @@ def build(T, gs, nxt):
             A(act(H("Va", h, 512 * q, 512 * q + 512), T.dif[:, :], AF.Abs), 512, ["dif" + hs], ["Va%s%d" % (hs, q)], use=dx)
         fns = [mm(T.sm[:, 0:104], A0("w7"), A0("cpad"), True, False)]
         for w in range(12):
-            fns.append(mm(T.sm[:, 12 - w:104:13], H("Va", h, 128 * w, 128 * w + 128), A0("G1"), False, w == 11))
-        tx = P(fns, 104 + 768, ["w7", "cpad", "G1"] + ["Va%s%d" % (hs, q) for q in range(3)], ["S" + hs], acq="sm")
+            fns.append(mm(T.sm[:, 12 - w:104:13], T.Vb[:, 128 * h:128 * h + 128, w] if h in EY else H("Va", h, 128 * w, 128 * w + 128), A0("G1"),
+                          False, w == 11))
+        tx = P(fns, 104 + 768, ["w7", "cpad", "G1"] + (["Vb%s%d" % (hs, b) for b in range(4)] if h in EY else ["Va%s%d" % (hs, q) for q in range(3)]),
+               ["S" + hs], acq="sm")
         V(ts(H("nx", h), T.sm[:, 0:104], 820.0, None, Op.is_le), 104, ["S" + hs], ["nx" + hs], use=tx)
         V(scan(H("ns", h), A0("ONE"), H("nx", h), Op.add, Op.mult), 104, ["ONE", "nx" + hs], ["ns" + hs])
         V(cp(H("Xn", h, 0, 128, 16), H("ns", h, 12, None, 13)), 8, ["ns" + hs, "Xn" + hs], ["Xn" + hs])
@@ -360,21 +396,29 @@ def build(T, gs, nxt):
                ["Ih", "Qc", "nsb" + hs] + ["Wu%d" % u for u in range(4)], ["Q" + hs], acq="sm")
         V(cp(H("tof", h), T.sm[:, 0:32]), 32, ["Q" + hs], ["tof" + hs], use=tx)
         to = T.ts[:, 1024 * t + 512 * h:1024 * t + 512 * h + 512]
-        A(act(to, H("v2", h).indirect(H("tof", h))), 512 * 1.5, YK("v2", h) + ["tof" + hs], ["ts%d%d" % (t, h)])
+        A(act(to, H("v2", h, 0, 2048).indirect(H("tof", h))), 512 * 1.5, YK("v2", h) + ["tof" + hs], ["ts%d%d" % (t, h)])
         send(t, "T", h, T["tl%d" % (t + 1)][:, 128 * h:128 * h + 128, :], to, "ts%d%d" % (t, h))
 
     for t in range(NV):
+        tag[0] = ("L", 0)
         gatherlist(t)
         for h in range(2):
+            tag[0] = ("F", h)
             front(t, h)
         for h in range(2):
+            tag[0] = ("H", h)
             heavy(t, h)
+            tag[0] = ("D", h)
             decide(t, h)
-            fresh(t, h)
         if t < NV - 1:
+            tag[0] = ("C", 0)
             counts(t)
         for h in range(2):
+            tag[0] = ("N", h)
+            fresh(t, h)
+            tag[0] = ("E", h)
             finish(t, h)
+    tag[0] = ("O", 0)
 
     st = "st%d" % (NV % 2)
     V(ts(A0("li"), A0("LF"), T.al[:, 4 * NV - 4:4 * NV - 3], None, Op.subtract), 16, ["LF", "A%d" % (NV - 1)], ["li"])
@@ -412,6 +456,7 @@ def schedule(ops):
     pr = [0.0] * n
     for i in range(n - 1, -1, -1):
         pr[i] = ops[i]["cost"] + 0.04 + max([pr[k] for k in succ[i]], default=0.0)
+    pr = [pr[i] + BONUS.get(ops[i]["tag"], 0.0) for i in range(n)]
     left = [len(o["deps"]) for o in ops]
     members = {}
     for i, o in enumerate(ops):
@@ -442,7 +487,7 @@ def schedule(ops):
                 cand.append((est, i))
             if not cand:
                 continue
-            lo = min(c[0] for c in cand) + 0.05
+            lo = min(c[0] for c in cand) + WIN
             est, i = max((c for c in cand if c[0] <= lo), key=lambda c: pr[c[1]])
             if best is None or est < best[0]:
                 best = (est, i, e)
@@ -482,7 +527,7 @@ def emit(ops, order, T, gs):
     def after(e, i, raw):
         o = ops[i]
         sem, val, clk = done[i]
-        if o["eng"] == e and not raw:
+        if o["eng"] == e == "p" and not raw:
             return
         if know[e].get(sem, 0) >= val:
             return

@@ -3,15 +3,16 @@ from concourse.mybir import dt, AluOpType as Op, ActivationFunctionType as AF
 
 NV = 8
 J = 13
-JA = (11, 9)
+JA = (11, 11)
 NM = 4
 GP = 4
 EY = (0, 1)
-ZP = (0,)
 VG = (("v2", 1, 1), ("y2", 0, 1), ("y2", 0, 3), ("v2", 1, 3))
+VG0, VGL = VG, VG
 WIN = 0.02
 BONUS = {("F", 0): -96.8, ("H", 0): -145.4, ("D", 0): 78.0, ("N", 0): 229.2, ("E", 0): -208.8, ("L", 0): 199.4, ("C", 0): -76.6,
          ("F", 1): -136.4, ("H", 1): -204.6, ("D", 1): -162.2, ("N", 1): 211.4, ("E", 1): -111.2}
+OPB = {}
 MAGIC = 201326592.0
 EARLY, LATE = 37528.0, 1.0e9
 
@@ -30,7 +31,7 @@ SCRATCH = {
     "sh": ("sbuf", [128, 32], I32), "q1": ("sbuf", [128, 32], I32), "q2": ("sbuf", [128, 32], I32), "l5": ("sbuf", [128, 16], I32),
     "w9": ("sbuf", [128, 128], F32), "w18": ("sbuf", [128, 128], F32), "mu": ("sbuf", [128, 32], F32), "shf": ("sbuf", [128, 8], F32),
     "gf": ("sbuf", [128, 8], F32), "gr": ("sbuf", [128, 104], F32), "sg1": ("sbuf", [128, 104], F32), "sg2": ("sbuf", [128, 104], F32),
-    "B32": ("sbuf", [128, 128], F32), "I32": ("sbuf", [128, 128], F32), "Bb": ("sbuf", [128, 128], BF), "Ib": ("sbuf", [128, 128], BF), "I16": ("sbuf", [128, 128], BF),
+    "B32": ("sbuf", [128, 128], F32), "Bb": ("sbuf", [128, 128], BF), "Ib": ("sbuf", [128, 128], BF), "I16": ("sbuf", [128, 128], BF),
     "Im": ("sbuf", [128, 128], BF), "Ih": ("sbuf", [128, 128], F16), "W0": ("sbuf", [128, 128], F16), "W1": ("sbuf", [128, 128], F16),
     "Wu": ("sbuf", [128, 512], BF), "G1": ("sbuf", [128, 8], BF), "G32": ("sbuf", [128, 8], BF), "Z": ("sbuf", [128, 8, 32], BF),
     "RT0": ("sbuf", [128, 104], BF), "RT1": ("sbuf", [128, 104], BF), "cj": ("sbuf", [128, 104], BF), "cpad": ("sbuf", [128, 104], BF), "KD": ("sbuf", [128, 104], F32),
@@ -60,11 +61,12 @@ SEMAPHORES.remove("rA%d" % NV)
 
 
 def build(T, gs, nxt):
-    ops, lastw, readers, accs, tag = [], {}, {}, {}, [("I", 0)]
+    ops, lastw, readers, accs, nums, tag = [], {}, {}, {}, {}, [("I", 0, 0)]
 
     def add(eng, fns, cost, rd=(), wr=(), acc=None, acq=None, use=None, after=(), pin=None):
         i = len(ops)
         deps = {}
+        nums[tag[0]] = nums.get(tag[0], -1) + 1
         for k in rd:
             for o in ([lastw[k]] if k in lastw else []) + accs.get(k, []):
                 deps[o] = True
@@ -81,7 +83,7 @@ def build(T, gs, nxt):
             deps[o] = deps.get(o, False)
         if acq is not None:
             use = i
-        ops.append(dict(eng=eng, fns=fns, cost=cost, deps=deps, acq=acq, use=use, sym=pin, tag=tag[0], wr=tuple(wr)))
+        ops.append(dict(eng=eng, fns=fns, cost=cost, deps=deps, acq=acq, use=use, sym=pin, bonus=BONUS.get(tag[0][:2], 0.0) + OPB.get(tag[0][:2] + (nums[tag[0]],), 0.0), tag=tag[0], num=nums[tag[0]], wr=tuple(wr)))
         return i
 
     v, s, p, g = gs["v"], gs["a"], gs["p"], gs["q"]
@@ -93,7 +95,7 @@ def build(T, gs, nxt):
         return add("a", [fn], 0.065 + c * 0.001, rd, wr, **kw)
 
     def P(fns, c, rd=(), wr=(), **kw):
-        return add("p", fns, c * 0.0006, rd, wr, **kw)
+        return add("p", fns, c * 0.0005, rd, wr, **kw)
 
     def mm(out, l, r, start=True, stop=True):
         return lambda last: p.matmul(out, l, r, start, stop or last)
@@ -115,8 +117,8 @@ def build(T, gs, nxt):
     def scan(out, a, b, o0, o1):
         return lambda last: v.tensor_tensor_scan(out, a, b, 0.0, o0, o1)
 
-    def load(out, a, sem, key, lat):
-        return add("d", [lambda last: gs["d"].dma_start(out, a)], lat, (), [key], pin=(sem, 16))
+    def load(out, a, sem, key, lat, after=()):
+        return add("d", [lambda last: gs["d"].dma_start(out, a)], lat, (), [key], pin=(sem, 16), after=after)
 
     def H(name, h, a=0, b=None, step=None):
         n = _HALF[name][0]
@@ -135,7 +137,7 @@ def build(T, gs, nxt):
     iota("iL", [[16, 16]], 0, 0)
     iota("iC", [[1, 8], [0, 13]], 0, 0)
     iota("iJ", [[0, 8], [1, 13]], 0, 0)
-    iota("i64", [[64, 32]], -3, 0)
+    iota("i64", [[64, 32]], 6, 0)
 
     def C(fn, c, rd, wr):
         return V(fn, c, rd, [wr])
@@ -155,14 +157,11 @@ def build(T, gs, nxt):
     C(tt(T.R8[:, :], T.iP[0:8, :], T.qg[0:8, :], Op.is_equal), 256, ["iP", "qg"], "R8")
     A(act(A0("Bb"), A0("B32")), 128, ["B32"], ["Bb"])
     C(tt(A0("Ib"), A0("iP"), A0("iQ"), Op.is_equal), 256, ["iP", "iQ"], "Ib")
-    A(act(A0("I32"), A0("Ib")), 128, ["Ib"], ["I32"])
     A(act(A0("I16"), A0("Ib"), scale=16.0), 128, ["Ib"], ["I16"])
     A(act(A0("Im"), A0("Ib"), scale=-1.0), 128, ["Ib"], ["Im"])
     C(cp(A0("Ih"), A0("Ib")), 64, ["Ib"], "Ih")
-    C(ts(A0("w9"), A0("qm"), 9.5, None, Op.add), 128, ["qm"], "w9")
-    C(ts(A0("w18"), A0("qm"), 18.5, None, Op.add), 128, ["qm"], "w18")
+    C(ts(A0("w9"), A0("qm"), 0.5, None, Op.add), 128, ["qm"], "w9")
     C(tt(A0("W0"), A0("w9"), A0("B32"), Op.mult), 256, ["w9", "B32"], "W0")
-    C(tt(A0("W1"), A0("w18"), A0("B32"), Op.mult), 256, ["w18", "B32"], "W1")
     C(tt(A0("gf"), T.pg[:, 0:8], T.iQ[:, 0:8], Op.is_equal), 16, ["pg", "iQ"], "gf")
     C(cp(A0("G1"), A0("gf")), 8, ["gf"], "G1")
     C(ts(A0("G32"), A0("gf"), 32.0, None, Op.mult), 8, ["gf"], "G32")
@@ -189,7 +188,7 @@ def build(T, gs, nxt):
     fill("w7", 2.0 ** -7, 64)
     fill("c185", -18.5, 64)
     fill("cm16", -16.0, 64)
-    fill("c3", 3.0, 64)
+    fill("c3", -6.0, 64)
     fill("c205", 205.0, 8)
     fill("ONE", 1.0, 104)
     for h in EY:
@@ -201,7 +200,7 @@ def build(T, gs, nxt):
     C(cp(T.z0f[:, :], T.z0s[:, :]), 256, ["z0s"], "z0f")
     tx = P([mm(T.sm[:, 0:256], T.R8[:, :], T.z0f[:, :])], 1024, ["R8", "z0f"], ["sm"], acq="sm")
     for h in range(2):
-        V(cp(T.zb[:, 128 * h:128 * h + 128], T.sm[:, 128 * h:128 * h + 128]), 128, ["sm"], ["z0%d" % h], use=tx)
+        V(ts(T.zb[:, 128 * h:128 * h + 128], T.sm[:, 128 * h:128 * h + 128], 9.0, None, Op.add), 128, ["sm"], ["z0%d" % h], use=tx)
     C(cp(A0("st0"), A0("s0s")), 256, ["s0s"], "st0_0")
     lastw["st0_1"] = lastw["st0_0"]
     C(ts(A0("dg1"), A0("cfs"), 2.0, 1.0, Op.mult, Op.add), 256, ["cfs"], "dg1")
@@ -254,10 +253,10 @@ def build(T, gs, nxt):
         V(ts(H("fm", h), H("fi", h), 4095, None, Op.bitwise_and), 128, ["fi" + hs], ["fm" + hs])
         V(cp(H("of", h), H("fm", h)), 128, ["fm" + hs], ["of" + hs])
 
-    def samples(h, buf):
+    def samples(t, h, buf):
         hs, k = str(h), 128 // GP
         for q in range(GP):
-            on_v = (buf, h, q) in VG
+            on_v = (buf, h, q) in (VG0 if t == 0 else VGL if t == NV - 1 else VG)
             (V if on_v else A)((cp if on_v else act)(H(buf, h, 16 * k * q, 16 * k * q + 16 * k), T.x[:, :].indirect(H("of", h, k * q, k * q + k))),
                                16 * k * 1.5, ["x", "of" + hs], [buf + hs + "_%d" % q])
     YK = lambda b, h: [b + str(h) + "_%d" % q for q in range(GP)]
@@ -267,10 +266,10 @@ def build(T, gs, nxt):
         X = T.vt[:, 256 * h:256 * h + 128]
         dn = "dg%d" % (t % 2)
         V(tt(X, zref(t, h), T.sg[:, c0:c0 + 128], Op.subtract), 256, ["z%d%d" % (t, h), "sg"], ["vX" + hs])
-        V(ts(H("cmp", h), X, 0.0, None, Op.is_ge), 128, ["vX" + hs], ["cmp" + hs])
+        V(ts(H("cmp", h), X, 9.0, None, Op.is_ge), 128, ["vX" + hs], ["cmp" + hs])
         V(tt(H("Hb", h), X, T[dn][:, c0:c0 + 128], Op.mult), 128, ["vX" + hs, dn], ["Hb" + hs])
         select(t, h, "W0", 0)
-        samples(h, "y2")
+        samples(t, h, "y2")
 
     def heavy(t, h):
         hs = str(h)
@@ -321,25 +320,19 @@ def build(T, gs, nxt):
         Y = T.vt[:, 256 * h + 128:256 * h + 256]
         dn, sn = "dg%d" % (t % 2), "st%d" % ((t + 1) % 2)
         zk = "z%d%d" % (t, h)
-        if h in ZP:
-            tx = P([mm(T.sm[:, 0:128], A0("w7"), A0("cm16"), True, False), mm(T.sm[:, 0:128], A0("I32"), zref(t, h), False, False),
-                    mm(T.sm[:, 0:128], H("Xr", h, 0, 128), A0("I16"), False, True)], 768, ["w7", "cm16", "I16", "I32", "Xr" + hs, zk], ["tz" + hs], acq="sm")
-            A(act(H("zp", h), T.sm[:, 0:128], AF.Relu), 128, ["tz" + hs], ["zp" + hs], use=tx)
-            tx = P([mm(T.sm[:, 128:256], H("Xr", h, 128, 256), A0("Ib"))], 128, ["Ib", "Xe" + hs], ["td" + hs], acq="sm")
-            V(tt(H("dge", h), T.sm[:, 128:256], H("geb", h), Op.mult), 128, ["td" + hs, "geb" + hs], ["dge" + hs], use=tx)
-        else:
+        if True:
             tx = P([mm(T.sm[:, 0:128], A0("w7"), A0("cm16"), True, False), mm(T.sm[:, 0:128], H("Xr", h, 0, 128), A0("I16"), False, True),
                     mm(T.sm[:, 128:256], H("Xr", h, 128, 256), A0("Ib"))], 384, ["w7", "cm16", "I16", "Ib", "Xr" + hs, "Xe" + hs], ["tz" + hs], acq="sm")
             V(tt(Y, zref(t, h), T.sm[:, 0:128], Op.add), 128, [zk, "tz" + hs], ["vY" + hs], use=tx)
             V(tt(H("dge", h), T.sm[:, 128:256], H("geb", h), Op.mult), 128, ["tz" + hs, "geb" + hs], ["dge" + hs], use=tx)
-            V(ts(H("zp", h), Y, 0.0, None, Op.max), 128, ["vY" + hs], ["zp" + hs])
+            V(ts(H("zp", h), Y, 9.0, 9.0, Op.max, Op.add), 128, ["vY" + hs], ["zp" + hs])
         V(tt(X, H("zp", h), T.sg[:, c0:c0 + 128], Op.subtract), 256, ["zp" + hs, "sg"], ["vX" + hs])
-        V(ts(H("cmp", h), X, 0.0, None, Op.is_ge), 128, ["vX" + hs], ["cmp" + hs])
+        V(ts(H("cmp", h), X, 18.0, None, Op.is_ge), 128, ["vX" + hs], ["cmp" + hs])
         V(tt(Y, X, H("dge", h), Op.subtract), 128, ["vX" + hs, "dge" + hs], ["vY" + hs])
         V(tt(H("Hb", h), Y, T[dn][:, c0:c0 + 128], Op.mult), 128, ["vY" + hs, dn], ["Hb" + hs])
         V(tt(T[sn][:, c0:c0 + 128], H("dge", h), T.sg[:, c0:c0 + 128], Op.add), 256, ["dge" + hs, "sg"], ["%s_%d" % (sn, h)])
-        select(t, h, "W1", 1)
-        samples(h, "v2")
+        select(t, h, "W0", 1)
+        samples(t, h, "v2")
 
     def counts(t):
         tx = P([mm(T.sm[:, 0:1], H("Xr", 0, 0, 128), T.c205[:, 0:1], True, False), mm(T.sm[:, 0:1], H("Xr", 1, 0, 128), T.c205[:, 0:1], False, True)],
@@ -371,8 +364,8 @@ def build(T, gs, nxt):
             fns = []
             for w in range(4):
                 m = 4 + 4 * q + w
-                fns += [mm(T.dif[:, 128 * w:128 * w + 128], A0("Ib"), H("v2", h, m, None, 16), True, False),
-                        mm(T.dif[:, 128 * w:128 * w + 128], A0("Im"), H("v2", h, m - 1, None, 16), False, True)]
+                fns += [mm(T.dif[:, 128 * w:128 * w + 128], A0("Ib"), H("v2", h, m, 2048, 16), True, False),
+                        mm(T.dif[:, 128 * w:128 * w + 128], A0("Im"), H("v2", h, m - 1, 2048, 16), False, True)]
             dx = P(fns, 1024, YK("v2", h) + ["Ib", "Im"], ["dif" + hs], acq="dif")
             A(act(H("Va", h, 512 * q, 512 * q + 512), T.dif[:, :], AF.Abs), 512, ["dif" + hs], ["Va%s%d" % (hs, q)], use=dx)
         fns = [mm(T.sm[:, 0:104], A0("w7"), A0("cpad"), True, False)]
@@ -381,8 +374,8 @@ def build(T, gs, nxt):
                           False, w == 11))
         tx = P(fns, 104 + 768, ["w7", "cpad", "G1"] + (["Vb%s%d" % (hs, b) for b in range(4)] if h in EY else ["Va%s%d" % (hs, q) for q in range(3)]),
                ["S" + hs], acq="sm")
-        V(ts(H("nx", h), T.sm[:, 0:104], 820.0, None, Op.is_le), 104, ["S" + hs], ["nx" + hs], use=tx)
-        V(scan(H("ns", h), A0("ONE"), H("nx", h), Op.add, Op.mult), 104, ["ONE", "nx" + hs], ["ns" + hs])
+        A(act(H("nx", h), T.sm[:, 0:104], AF.Relu, 26256.0, -32.0), 104, ["S" + hs], ["nx" + hs], use=tx)
+        V(scan(H("ns", h), A0("ONE"), H("nx", h), Op.add, Op.min), 104, ["ONE", "nx" + hs], ["ns" + hs])
         V(cp(H("Xn", h, 0, 128, 16), H("ns", h, 12, None, 13)), 8, ["ns" + hs, "Xn" + hs], ["Xn" + hs])
         V(scan(H("Xnr", h), T.RD[:, 0:128], H("Xn", h), Op.mult, Op.add), 64, ["RD", "Xn" + hs], ["Xnr" + hs])
         tx = P([mm(T.sm[:, 0:128], A0("w7"), A0("c3"), True, False), mm(T.sm[:, 0:128], H("Xnr", h), A0("Ib"), False, True)], 256,
@@ -400,25 +393,25 @@ def build(T, gs, nxt):
         send(t, "T", h, T["tl%d" % (t + 1)][:, 128 * h:128 * h + 128, :], to, "ts%d%d" % (t, h))
 
     for t in range(NV):
-        tag[0] = ("L", 0)
+        tag[0] = ("L", 0, t)
         gatherlist(t)
         for h in range(2):
-            tag[0] = ("F", h)
+            tag[0] = ("F", h, t)
             front(t, h)
         for h in range(2):
-            tag[0] = ("H", h)
+            tag[0] = ("H", h, t)
             heavy(t, h)
-            tag[0] = ("D", h)
+            tag[0] = ("D", h, t)
             decide(t, h)
         if t < NV - 1:
-            tag[0] = ("C", 0)
+            tag[0] = ("C", 0, t)
             counts(t)
         for h in range(2):
-            tag[0] = ("N", h)
+            tag[0] = ("N", h, t)
             fresh(t, h)
-            tag[0] = ("E", h)
+            tag[0] = ("E", h, t)
             finish(t, h)
-    tag[0] = ("O", 0)
+    tag[0] = ("O", 0, 0)
 
     st = "st%d" % (NV % 2)
     V(ts(A0("li"), A0("LF"), T.al[:, 4 * NV - 4:4 * NV - 3], None, Op.subtract), 16, ["LF", "A%d" % (NV - 1)], ["li"])
@@ -431,7 +424,8 @@ def build(T, gs, nxt):
     store(T.ys[:, :], T.ysb[:, :], ["ysb"])
     for h in range(2):
         c = 256 * (NV - 1) + 128 * h
-        store(T.yz[:, 128 * h:128 * h + 128], T.zl[0:128:16, c:c + 128], ["z%d%d" % (NV, h)])
+        V(ts(T.zb[:, 128 * h:128 * h + 128], T.zl[:, c:c + 128], -9.0, None, Op.add), 128, ["z%d%d" % (NV, h)], ["z0%d" % h])
+        store(T.yz[:, 128 * h:128 * h + 128], T.zb[0:128:16, 128 * h:128 * h + 128], ["z0%d" % h])
     fin = []
     for h in range(2):
         for a in range(4):
@@ -456,7 +450,7 @@ def schedule(ops):
     pr = [0.0] * n
     for i in range(n - 1, -1, -1):
         pr[i] = ops[i]["cost"] + 0.04 + max([pr[k] for k in succ[i]], default=0.0)
-    pr = [pr[i] + BONUS.get(ops[i]["tag"], 0.0) for i in range(n)]
+    pr = [pr[i] + ops[i]["bonus"] for i in range(n)]
     left = [len(o["deps"]) for o in ops]
     members = {}
     for i, o in enumerate(ops):

import numpy as np
from concourse.mybir import dt, AluOpType as Op, ActivationFunctionType as AF

NV = 8
J = 13
JA = (11, 11)
NM = 4
GP = 4
EY = (0, 1)
VG = (("v2", 1, 1), ("y2", 0, 1), ("y2", 0, 3), ("v2", 1, 3))
VG0, VGL = VG, VG
WIN = 0.02
BONUS = {("F", 0): -96.8, ("H", 0): -145.4, ("D", 0): 78.0, ("N", 0): 229.2, ("E", 0): -208.8, ("L", 0): 199.4, ("C", 0): -76.6,
         ("F", 1): -136.4, ("H", 1): -204.6, ("D", 1): -162.2, ("N", 1): 211.4, ("E", 1): -111.2}
OPB = {}
MAGIC = 201326592.0
EARLY, LATE = 37528.0, 1.0e9

F32, BF, F16, I32, U16 = "float32", "bfloat16", "float16", "int32", "uint16"
SCRATCH = {
    "x": ("sbuf", [128, 4096], BF), "t0s": ("sbuf", [128, 1024], BF), "ytb": ("sbuf", [128, 1024], BF),
    "s0s": ("sbuf", [128, 256], I32), "cfs": ("sbuf", [128, 256], I32), "z0s": ("sbuf", [8, 256], I32), "z0f": ("sbuf", [8, 256], F32),
    "st0": ("sbuf", [128, 256], F32), "st1": ("sbuf", [128, 256], F32), "sg": ("sbuf", [128, 256], F32),
    "dg0": ("sbuf", [128, 256], F32), "dg1": ("sbuf", [128, 256], F32), "ysb": ("sbuf", [128, 256], F32),
    "zb": ("sbuf", [128, 256], F32), "zl": ("sbuf", [128, 8 * 256], F32), "zm": ("sbuf", [128, 8 * 256], F32),
    "al": ("sbuf", [128, 64], F32), "am": ("sbuf", [128, 64], F32),
    "li": ("sbuf", [128, 16], I32), "lm": ("sbuf", [128, 16], I32), "lu": ("sbuf", [128, 16], U16),
    "iP": ("sbuf", [128, 128], I32), "iQ": ("sbuf", [128, 128], I32), "iC": ("sbuf", [128, 104], I32), "iJ": ("sbuf", [128, 104], I32),
    "iL": ("sbuf", [128, 16], I32), "i64": ("sbuf", [128, 32], I32),
    "pg": ("sbuf", [128, 128], I32), "qg": ("sbuf", [128, 128], I32), "pm": ("sbuf", [128, 128], I32), "qm": ("sbuf", [128, 128], I32),
    "sh": ("sbuf", [128, 32], I32), "q1": ("sbuf", [128, 32], I32), "q2": ("sbuf", [128, 32], I32), "l5": ("sbuf", [128, 16], I32),
    "w9": ("sbuf", [128, 128], F32), "w18": ("sbuf", [128, 128], F32), "mu": ("sbuf", [128, 32], F32), "shf": ("sbuf", [128, 8], F32),
    "gf": ("sbuf", [128, 8], F32), "gr": ("sbuf", [128, 104], F32), "sg1": ("sbuf", [128, 104], F32), "sg2": ("sbuf", [128, 104], F32),
    "B32": ("sbuf", [128, 128], F32), "Bb": ("sbuf", [128, 128], BF), "Ib": ("sbuf", [128, 128], BF), "I16": ("sbuf", [128, 128], BF),
    "Im": ("sbuf", [128, 128], BF), "Ih": ("sbuf", [128, 128], F16), "W0": ("sbuf", [128, 128], F16), "W1": ("sbuf", [128, 128], F16),
    "Wu": ("sbuf", [128, 512], BF), "G1": ("sbuf", [128, 8], BF), "G32": ("sbuf", [128, 8], BF), "Z": ("sbuf", [128, 8, 32], BF),
    "RT0": ("sbuf", [128, 104], BF), "RT1": ("sbuf", [128, 104], BF), "cj": ("sbuf", [128, 104], BF), "cpad": ("sbuf", [128, 104], BF), "KD": ("sbuf", [128, 104], F32),
    "ONE": ("sbuf", [128, 104], F32), "RD": ("sbuf", [128, 128], BF), "Qc": ("sbuf", [128, 32], F16), "rp1": ("sbuf", [128, 8], F32),
    "LB": ("sbuf", [128, 16], F32), "LF": ("sbuf", [128, 16], F32), "R8": ("sbuf", [8, 128], F32),
    "w7": ("sbuf", [128, 128], BF), "c185": ("sbuf", [128, 128], BF), "cm16": ("sbuf", [128, 128], BF), "c3": ("sbuf", [128, 128], BF),
    "c205": ("sbuf", [128, 8], BF),
    "yps": ("psum", [128, 128, 16], F32), "dif": ("psum", [128, 512], F32), "vt": ("psum", [128, 512], F32),
    "kb": ("psum", [128, 512], F32), "sm": ("psum", [128, 512], F32),
}
_HALF = {"cmp": (128, BF), "geb": (128, BF), "Hb": (128, F32), "oH": (128, F32), "oD": (128, F16), "fi": (128, I32), "fm": (128, I32),
         "of": (128, U16), "y2": (2048, BF), "v2": (2064, BF), "Va": (1536, BF), "ks": (104, F32), "rr": (8, F32), "dd": (8, F32),
         "Xs": (256, BF), "Xr": (256, BF), "dge": (128, F32), "zp": (128, F32), "nx": (104, F32), "ns": (104, F32), "Xn": (128, BF),
         "Xnr": (128, BF), "nsb": (128, BF), "tof": (32, U16), "Ma": (512 * (J - min(JA)), BF)}
for _n, (_c, _d) in _HALF.items():
    SCRATCH[_n] = ("sbuf", [128, 2 * _c], _d)
for _m in range(NM):
    SCRATCH["mb%d" % _m] = ("sbuf", [128, 128, 4], BF)
SCRATCH["Vb"] = ("sbuf", [128, 256, 12], BF)
SCRATCH["ts"] = ("sbuf", [128, NV * 1024], BF)
for _t in range(NV + 1):
    SCRATCH["tl%d" % _t] = ("sbuf", [128, 256, 4], BF)
SEMAPHORES = ["v", "a", "p", "q", "lx", "ls", "lc", "lz", "lt", "loc", "sto"]
for _t in range(1, NV + 1):
    SEMAPHORES += ["rA%d" % _t, "rz%d0" % _t, "rz%d1" % _t, "rT%d0" % _t, "rT%d1" % _t]
SEMAPHORES.remove("rA%d" % NV)


def build(T, gs, nxt):
    ops, lastw, readers, accs, nums, tag = [], {}, {}, {}, {}, [("I", 0, 0)]

    def add(eng, fns, cost, rd=(), wr=(), acc=None, acq=None, use=None, after=(), pin=None):
        i = len(ops)
        deps = {}
        nums[tag[0]] = nums.get(tag[0], -1) + 1
        for k in rd:
            for o in ([lastw[k]] if k in lastw else []) + accs.get(k, []):
                deps[o] = True
            readers.setdefault(k, []).append(i)
        if acc is not None:
            deps[lastw[acc]] = deps.get(lastw[acc], False)
            accs.setdefault(acc, []).append(i)
        for k in wr:
            for o in readers.get(k, []) + ([lastw[k]] if k in lastw else []) + accs.get(k, []):
                if o != i:
                    deps[o] = deps.get(o, False)
            lastw[k], readers[k], accs[k] = i, [], []
        for o in after:
            deps[o] = deps.get(o, False)
        if acq is not None:
            use = i
        ops.append(dict(eng=eng, fns=fns, cost=cost, deps=deps, acq=acq, use=use, sym=pin, bonus=BONUS.get(tag[0][:2], 0.0) + OPB.get(tag[0][:2] + (nums[tag[0]],), 0.0), tag=tag[0], num=nums[tag[0]], wr=tuple(wr)))
        return i

    v, s, p, g = gs["v"], gs["a"], gs["p"], gs["q"]

    def V(fn, c, rd=(), wr=(), **kw):
        return add("v", [fn], 0.05 + max(64, c) * 0.001, rd, wr, **kw)

    def A(fn, c, rd=(), wr=(), **kw):
        return add("a", [fn], 0.065 + c * 0.001, rd, wr, **kw)

    def P(fns, c, rd=(), wr=(), **kw):
        return add("p", fns, c * 0.0005, rd, wr, **kw)

    def mm(out, l, r, start=True, stop=True):
        return lambda last: p.matmul(out, l, r, start, stop or last)

    def ts(out, a, s1, s2, o0, o1=None):
        if o1 is None:
            return lambda last: v.tensor_scalar(out, a, s1, None, o0)
        return lambda last: v.tensor_scalar(out, a, s1, s2, o0, o1)

    def tt(out, a, b, o):
        return lambda last: v.tensor_tensor(out, a, b, o)

    def cp(out, a):
        return lambda last: v.tensor_copy(out, a)

    def act(out, a, f=AF.Copy, bias=0.0, scale=1.0):
        return lambda last: s.activation(out, a, f, bias=bias, scale=scale)

    def scan(out, a, b, o0, o1):
        return lambda last: v.tensor_tensor_scan(out, a, b, 0.0, o0, o1)

    def load(out, a, sem, key, lat, after=()):
        return add("d", [lambda last: gs["d"].dma_start(out, a)], lat, (), [key], pin=(sem, 16), after=after)

    def H(name, h, a=0, b=None, step=None):
        n = _HALF[name][0]
        return T[name][:, n * h + a: n * h + (n if b is None else b): (step or 1)]

    load(T.z0s[:, :], T.z0[:, :], "lz", "z0s", 2.5)
    load(T.s0s[:, :], T.s0[:, :], "ls", "s0s", 3.0)
    load(T.cfs[:, :], T.cf[:, :], "lc", "cfs", 3.5)
    load(T.x[:, :], T.xl[:, :], "lx", "x", 9.0)
    load(T.t0s[:, :], T.t0[:, :], "lt", "t0s", 10.0)

    def iota(name, pat, base, cm):
        add("q", [lambda last: g.iota(T[name][:, :], pat, base, cm)], 0.4, (), [name])
    iota("iP", [[0, 128]], 0, 1)
    iota("iQ", [[1, 128]], 0, 0)
    iota("iL", [[16, 16]], 0, 0)
    iota("iC", [[1, 8], [0, 13]], 0, 0)
    iota("iJ", [[0, 8], [1, 13]], 0, 0)
    iota("i64", [[64, 32]], 6, 0)

    def C(fn, c, rd, wr):
        return V(fn, c, rd, [wr])

    def fill(name, val, c):
        C(lambda last: v.memset(T[name][:, :], val) if name != "Z" else v.memset(T.Z[:, :, :], val), c, [], name)
    A0 = lambda n, a=0, b=None: T[n][:, a:b] if b is not None else T[n][:, :]
    C(ts(A0("pm"), A0("iP"), 15, None, Op.bitwise_and), 128, ["iP"], "pm")
    C(tt(A0("LB"), A0("iL"), A0("pm", 0, 16), Op.add), 16, ["iL", "pm"], "LB")
    C(ts(A0("l5"), A0("LB"), 5.0, None, Op.mult), 16, ["LB"], "l5")
    C(ts(A0("LF"), A0("LB"), 205.0, None, Op.mult), 16, ["LB"], "LF")
    C(ts(A0("qg"), A0("iQ"), 4, None, Op.arith_shift_right), 128, ["iQ"], "qg")
    C(ts(A0("pg"), A0("iP"), 4, None, Op.arith_shift_right), 128, ["iP"], "pg")
    C(ts(A0("qm"), A0("iQ"), 15, None, Op.bitwise_and), 128, ["iQ"], "qm")
    C(ts(T.rp1[:, 0:1], T.pm[:, 0:1], 1.0, None, Op.add), 1, ["pm"], "rp1")
    C(tt(A0("B32"), A0("pg"), A0("qg"), Op.is_equal), 256, ["pg", "qg"], "B32")
    C(tt(T.R8[:, :], T.iP[0:8, :], T.qg[0:8, :], Op.is_equal), 256, ["iP", "qg"], "R8")
    A(act(A0("Bb"), A0("B32")), 128, ["B32"], ["Bb"])
    C(tt(A0("Ib"), A0("iP"), A0("iQ"), Op.is_equal), 256, ["iP", "iQ"], "Ib")
    A(act(A0("I16"), A0("Ib"), scale=16.0), 128, ["Ib"], ["I16"])
    A(act(A0("Im"), A0("Ib"), scale=-1.0), 128, ["Ib"], ["Im"])
    C(cp(A0("Ih"), A0("Ib")), 64, ["Ib"], "Ih")
    C(ts(A0("w9"), A0("qm"), 0.5, None, Op.add), 128, ["qm"], "w9")
    C(tt(A0("W0"), A0("w9"), A0("B32"), Op.mult), 256, ["w9", "B32"], "W0")
    C(tt(A0("gf"), T.pg[:, 0:8], T.iQ[:, 0:8], Op.is_equal), 16, ["pg", "iQ"], "gf")
    C(cp(A0("G1"), A0("gf")), 8, ["gf"], "G1")
    C(ts(A0("G32"), A0("gf"), 32.0, None, Op.mult), 8, ["gf"], "G32")
    fill("Z", 0.0, 256)
    for k in range(4):
        C(ts(T.Z[:, :, 16 + k], A0("gf"), -16.0, None, Op.mult), 8, ["gf", "Z"], "Z")
    C(ts(A0("cj"), A0("iJ"), 10.0, None, Op.add), 104, ["iJ"], "cj")
    C(ts(A0("cpad"), A0("iJ"), 0.0, 1000.0, Op.is_equal, Op.mult), 104, ["iJ"], "cpad")
    C(ts(A0("KD"), A0("iJ"), 0.0, LATE, Op.is_equal, Op.mult), 104, ["iJ"], "KD")
    C(tt(A0("gr"), T.pg[:, 0:104], A0("iC"), Op.is_equal), 208, ["pg", "iC"], "gr")
    for h in range(2 if JA[0] != JA[1] else 1):
        C(ts(A0("sg1"), A0("iJ"), float(JA[h]), 32.0, Op.is_ge, Op.mult), 104, ["iJ"], "sg1")
        C(ts(A0("sg2"), A0("sg1"), -16.0, None, Op.add), 104, ["sg1"], "sg2")
        C(tt(A0("RT%d" % h), A0("sg2"), A0("gr"), Op.mult), 208, ["sg2", "gr"], "RT%d" % h)
    RT = ["RT0", "RT%d" % (JA[0] != JA[1])]
    C(ts(T.RD[:, 0:128], A0("qm"), 0.0, None, Op.is_gt), 128, ["qm"], "RD")
    C(ts(A0("sh"), T.pm[:, 0:32], 2, None, Op.arith_shift_right), 32, ["pm"], "sh")
    C(ts(A0("q1"), A0("sh"), 12.0, None, Op.mult), 32, ["sh"], "q1")
    C(tt(A0("q2"), A0("q1"), T.pm[:, 0:32], Op.add), 64, ["q1", "pm"], "q2")
    C(tt(A0("Qc"), A0("q2"), A0("i64"), Op.add), 64, ["q2", "i64"], "Qc")
    for u in range(4):
        C(ts(T.mu[:, 8 * u:8 * u + 1], T.sh[:, 0:1], float(u), None, Op.is_equal), 1, ["sh"], "mu%d" % u)
        C(ts(T.Wu[:, 128 * u:128 * u + 128], A0("Ib"), T.mu[:, 8 * u:8 * u + 1], None, Op.mult), 64, ["Ib", "mu%d" % u], "Wu%d" % u)
    fill("w7", 2.0 ** -7, 64)
    fill("c185", -18.5, 64)
    fill("cm16", -16.0, 64)
    fill("c3", -6.0, 64)
    fill("c205", 205.0, 8)
    fill("ONE", 1.0, 104)
    for h in EY:
        C((lambda h: lambda last: v.memset(H("v2", h, 2048, 2064), 0.0))(h), 16, [], "v2p%d" % h)
    for h in range(2):
        C((lambda h: lambda last: v.memset(H("Xs", h), 0.0))(h), 128, [], "Xs%d" % h)
        C((lambda h: lambda last: v.memset(H("Xn", h), 0.0))(h), 64, [], "Xn%d" % h)

    C(cp(T.z0f[:, :], T.z0s[:, :]), 256, ["z0s"], "z0f")
    tx = P([mm(T.sm[:, 0:256], T.R8[:, :], T.z0f[:, :])], 1024, ["R8", "z0f"], ["sm"], acq="sm")
    for h in range(2):
        V(ts(T.zb[:, 128 * h:128 * h + 128], T.sm[:, 128 * h:128 * h + 128], 9.0, None, Op.add), 128, ["sm"], ["z0%d" % h], use=tx)
    C(cp(A0("st0"), A0("s0s")), 256, ["s0s"], "st0_0")
    lastw["st0_1"] = lastw["st0_0"]
    C(ts(A0("dg1"), A0("cfs"), 2.0, 1.0, Op.mult, Op.add), 256, ["cfs"], "dg1")
    for h in range(2):
        for a in range(4):
            src = T.t0s[:, 256 * a + 128 * h:256 * a + 128 * h + 128]
            dst = T.tl0[:, 128 * h:128 * h + 128, a]
            if a < 2:
                V(cp(dst, src), 64, ["t0s"], ["T0%d" % h] if a == 0 else ["T0%d_%d" % (h, a)])
            else:
                A(act(dst, src), 128, ["t0s"], ["T0%d_%d" % (h, a)])

    mcount = [0]
    tx_of = {}

    def gatherlist(t):
        if t == 0:
            C(ts(A0("lm"), A0("l5"), 255, None, Op.bitwise_and), 16, ["l5"], "lm")
        else:
            b = T.al[:, 4 * t:4 * t + 1]
            if t == 1:
                V(ts(A0("li"), A0("LB"), b, None, Op.add), 16, ["LB", "A1"], ["li"])
            else:
                V(ts(A0("li"), A0("LB"), b, T.al[:, 4 * t - 4:4 * t - 3], Op.add, Op.subtract), 16, ["LB", "A%d" % t, "A%d" % (t - 1)], ["li"])
            C(ts(A0("lm"), A0("li"), 255, None, Op.bitwise_and), 16, ["li"], "lm")
        C(cp(A0("lu"), A0("lm")), 16, ["lm"], "lu")
        st, dn, do = "st%d" % (t % 2), "dg%d" % (t % 2), "dg%d" % ((t + 1) % 2)
        A(act(A0("sg"), T[st][:, :].indirect(T.lu[:, :])), 256 * 1.5, ["lu", st + "_0", st + "_1"], ["sg"])
        A(act(A0(dn), T[do][:, :].indirect(T.lu[:, :])), 256 * 1.5, ["lu", do], [dn])

    def zref(t, h):
        return T.zb[:, 128 * h:128 * h + 128] if t == 0 else T.zl[:, 256 * (t - 1) + 128 * h:256 * (t - 1) + 128 * h + 128]

    def select(t, h, W, tail):
        hs, c0 = str(h), 128 * h
        X = T.vt[:, 256 * h:256 * h + 128]
        Y = T.vt[:, 256 * h + 128:256 * h + 256]
        dn = "dg%d" % (t % 2)
        OHS, OK = (Y, "vY") if tail == 0 else (X, "vX")
        tx = P([mm(T.sm[:, 0:128], A0("Bb"), H("cmp", h))], 128, ["Bb", "cmp" + hs], ["cnt" + hs], acq="sm")
        V(ts(OHS, T.sm[:, 0:128], 1.0, T.rp1[:, 0:1], Op.max, Op.is_equal), 128, ["cnt" + hs, "rp1"], [OK + hs], use=tx)
        if tail == 0:
            V(ts(H("geb", h), T.sm[:, 0:128], T.rp1[:, 0:1], None, Op.is_le), 128, ["cnt" + hs, "rp1"], ["geb" + hs], use=tx)
        V(tt(H("oD", h), OHS, T[dn][:, c0:c0 + 128], Op.mult), 128, [OK + hs, dn], ["oD" + hs])
        V(tt(H("oH", h), OHS, H("Hb", h), Op.mult), 128, [OK + hs, "Hb" + hs], ["oH" + hs])
        tx = P([mm(T.sm[:, 0:128], A0("w7"), A0("c185"), True, False), mm(T.sm[:, 0:128], A0(W), H("oD", h), False, False)], 256,
               ["w7", "c185", W, "oD" + hs], ["F" + hs], acq="sm")
        P([mm(T.sm[:, 0:128], A0("B32"), H("oH", h), False, True)], 512, ["oH" + hs, "B32"], ["F" + hs], use=tx)
        V(cp(H("fi", h), T.sm[:, 0:128]), 128, ["F" + hs], ["fi" + hs], use=tx)
        V(ts(H("fm", h), H("fi", h), 4095, None, Op.bitwise_and), 128, ["fi" + hs], ["fm" + hs])
        V(cp(H("of", h), H("fm", h)), 128, ["fm" + hs], ["of" + hs])

    def samples(t, h, buf):
        hs, k = str(h), 128 // GP
        for q in range(GP):
            on_v = (buf, h, q) in (VG0 if t == 0 else VGL if t == NV - 1 else VG)
            (V if on_v else A)((cp if on_v else act)(H(buf, h, 16 * k * q, 16 * k * q + 16 * k), T.x[:, :].indirect(H("of", h, k * q, k * q + k))),
                               16 * k * 1.5, ["x", "of" + hs], [buf + hs + "_%d" % q])
    YK = lambda b, h: [b + str(h) + "_%d" % q for q in range(GP)]

    def front(t, h):
        hs, c0 = str(h), 128 * h
        X = T.vt[:, 256 * h:256 * h + 128]
        dn = "dg%d" % (t % 2)
        V(tt(X, zref(t, h), T.sg[:, c0:c0 + 128], Op.subtract), 256, ["z%d%d" % (t, h), "sg"], ["vX" + hs])
        V(ts(H("cmp", h), X, 9.0, None, Op.is_ge), 128, ["vX" + hs], ["cmp" + hs])
        V(tt(H("Hb", h), X, T[dn][:, c0:c0 + 128], Op.mult), 128, ["vX" + hs, dn], ["Hb" + hs])
        select(t, h, "W0", 0)
        samples(t, h, "y2")

    def heavy(t, h):
        hs = str(h)
        tl = T["tl%d" % t][:, 128 * h:128 * h + 128, :]
        ta = lambda a: T["tl%d" % t][:, 128 * h:128 * h + 128, a]
        TK = ["T%d%d" % (t, h)] + (["T0%d_%d" % (h, a) for a in (1, 2, 3)] if t == 0 else [])
        K = T.kb[:, 0:104]
        kx = P([mm(K, A0("w7"), A0("cj"), True, False)], 104, ["w7", "cj"] + YK("y2", h), ["K" + hs], acq="kb")
        P([mm(K, ta(a), A0(RT[h]), False, False) for a in range(4)], 416, TK + [RT[h]], [], acc="K" + hs, use=kx)
        P([mm(K, H("y2", h, m, None, 16), T.Z[:, :, 19 - m:32 - m], False, False) for m in range(16)], 1664,
          YK("y2", h) + ["Z"], [], acc="K" + hs, use=kx)
        yx = None
        for b in range(4):
            fill_b = [mm(T.yps[:, 32 * b:32 * b + 32, :], A0("Ib"), H("y2", h, 512 * b, 512 * b + 512))]
            y = P(fill_b, 512, ["y2%s_%d" % (hs, b * GP // 4), "Ib"], ["yps%s%d" % (hs, b)], **({"acq": "yps"} if b == 0 else {"use": yx, "after": [yx]}))
            yx = y if b == 0 else yx
        ja, jv = list(range(JA[h], J)), list(range(JA[h]))
        for x, j in enumerate(ja):
            dx = P([mm(T.dif[:, 128 * a:128 * a + 128], A0("Ib"), H("y2", h, j + a, None, 16), True, False) if w == 0 else
                    mm(T.dif[:, 128 * a:128 * a + 128], A0("Im"), ta(a), False, True) for a in range(4) for w in range(2)], 1024,
                   YK("y2", h) + TK + ["Ib", "Im"], ["dif" + hs], acq="dif")
            b = x
            A(act(H("Ma", h, 512 * b, 512 * b + 512), T.dif[:, :], AF.Relu), 512, ["dif" + hs], ["Ma%s%d" % (hs, b)], use=dx)
            P([mm(T.kb[:, j:104:13], H("Ma", h, 512 * b + 128 * a, 512 * b + 128 * a + 128), A0("G32"), False, False) for a in range(4)],
              256, ["Ma%s%d" % (hs, b), "G32"], [], acc="K" + hs, use=kx)
        for j in jv:
            n = mcount[0] % NM
            mcount[0] += 1
            M = T["mb%d" % n]
            V(tt(M[:, :, :], T.yps[:, :, j:j + 4], tl, Op.max), 512, ["yps%s%d" % (hs, b) for b in range(4)] + TK, ["mb%d" % n], use=yx)
            P([mm(T.kb[:, j:104:13], M[:, :, a], A0("G32"), False, False) for a in range(4)], 256, ["mb%d" % n, "G32"], [], acc="K" + hs, use=kx)
        V(scan(H("ks", h), A0("KD"), K, Op.max, Op.min), 104, ["K" + hs, "KD"], ["ks" + hs], use=kx)

    def decide(t, h):
        hs = str(h)
        best = H("ks", h, 12, None, 13)
        tie, dlt = H("Xs", h, 0, 128, 16), H("Xs", h, 128, 256, 16)
        V(ts(tie, best, EARLY, None, Op.is_lt), 8, ["ks" + hs, "Xs" + hs], ["Xt" + hs])
        V(scan(H("Xr", h, 0, 128), T.RD[:, 0:128], H("Xs", h, 0, 128), Op.mult, Op.add), 64, ["RD", "Xt" + hs], ["Xr" + hs])
        V(ts(H("rr", h), best, MAGIC, MAGIC, Op.add, Op.subtract), 8, ["ks" + hs], ["rr" + hs])
        V(tt(H("dd", h), H("rr", h), best, Op.subtract), 16, ["rr" + hs, "ks" + hs], ["dd" + hs])
        V(tt(dlt, H("dd", h), tie, Op.mult), 16, ["dd" + hs, "Xt" + hs], ["Xd" + hs])
        V(scan(H("Xr", h, 128, 256), T.RD[:, 0:128], H("Xs", h, 128, 256), Op.mult, Op.add), 64, ["RD", "Xd" + hs], ["Xe" + hs])

    def fresh(t, h):
        hs, c0 = str(h), 128 * h
        X = T.vt[:, 256 * h:256 * h + 128]
        Y = T.vt[:, 256 * h + 128:256 * h + 256]
        dn, sn = "dg%d" % (t % 2), "st%d" % ((t + 1) % 2)
        zk = "z%d%d" % (t, h)
        if True:
            tx = P([mm(T.sm[:, 0:128], A0("w7"), A0("cm16"), True, False), mm(T.sm[:, 0:128], H("Xr", h, 0, 128), A0("I16"), False, True),
                    mm(T.sm[:, 128:256], H("Xr", h, 128, 256), A0("Ib"))], 384, ["w7", "cm16", "I16", "Ib", "Xr" + hs, "Xe" + hs], ["tz" + hs], acq="sm")
            V(tt(Y, zref(t, h), T.sm[:, 0:128], Op.add), 128, [zk, "tz" + hs], ["vY" + hs], use=tx)
            V(tt(H("dge", h), T.sm[:, 128:256], H("geb", h), Op.mult), 128, ["tz" + hs, "geb" + hs], ["dge" + hs], use=tx)
            V(ts(H("zp", h), Y, 9.0, 9.0, Op.max, Op.add), 128, ["vY" + hs], ["zp" + hs])
        V(tt(X, H("zp", h), T.sg[:, c0:c0 + 128], Op.subtract), 256, ["zp" + hs, "sg"], ["vX" + hs])
        V(ts(H("cmp", h), X, 18.0, None, Op.is_ge), 128, ["vX" + hs], ["cmp" + hs])
        V(tt(Y, X, H("dge", h), Op.subtract), 128, ["vX" + hs, "dge" + hs], ["vY" + hs])
        V(tt(H("Hb", h), Y, T[dn][:, c0:c0 + 128], Op.mult), 128, ["vY" + hs, dn], ["Hb" + hs])
        V(tt(T[sn][:, c0:c0 + 128], H("dge", h), T.sg[:, c0:c0 + 128], Op.add), 256, ["dge" + hs, "sg"], ["%s_%d" % (sn, h)])
        select(t, h, "W0", 1)
        samples(t, h, "v2")

    def counts(t):
        tx = P([mm(T.sm[:, 0:1], H("Xr", 0, 0, 128), T.c205[:, 0:1], True, False), mm(T.sm[:, 0:1], H("Xr", 1, 0, 128), T.c205[:, 0:1], False, True)],
               128, ["Xr0", "Xr1", "c205"], ["Aps"], acq="sm")
        V(cp(T.am[:, 4 * t:4 * t + 1], T.sm[:, 0:1]), 1, ["Aps"], ["am%d" % t], use=tx)
        send(t, "A", None, T.al[:, 4 * t + 4:4 * t + 5], T.am[:, 4 * t:4 * t + 1], "am%d" % t)

    def send(t, kind, h, out, in_, key):
        sem = "r%s%d%s" % (kind, t + 1, "" if h is None else h)
        rid, pid, mask = nxt

        def fn(last):
            return g.remote_dma(out, in_, T.sem[sem], T.sem.loc, pid, rid, mask)
        i = add("q", [fn], 0.9, [key], [], pin=("send",))
        add("n", [], 3.0, [], ["%s%d%s" % (kind, t + 1, "" if h is None else h)], after=[i], pin=(sem, gs["neng"]))

    def finish(t, h):
        hs = str(h)
        ex = None
        for b in range(4 if h in EY else 0):
            e = P([mm(T.yps[:, 32 * b:32 * b + 32, :], A0("Ib"), H("v2", h, 512 * b + 1, 512 * b + 513), True, False),
                   mm(T.yps[:, 32 * b:32 * b + 32, :], A0("Im"), H("v2", h, 512 * b, 512 * b + 512), False, True)], 1024,
                  ["v2%s_%d" % (hs, k) for k in sorted({b * GP // 4, min(b + 1, 3) * GP // 4})] + ["v2p" + hs, "Ib", "Im"], ["yps%s%d" % (hs, b)],
                  **({"acq": "yps"} if b == 0 else {"use": ex, "after": [ex]}))
            ex = e if b == 0 else ex
            A(act(T.Vb[:, 128 * h + 32 * b:128 * h + 32 * b + 32, :], T.yps[:, 32 * b:32 * b + 32, 3:15], AF.Abs), 384,
              ["yps%s%d" % (hs, b)], ["Vb%s%d" % (hs, b)], use=ex)
        for q in range(0 if h in EY else 3):
            fns = []
            for w in range(4):
                m = 4 + 4 * q + w
                fns += [mm(T.dif[:, 128 * w:128 * w + 128], A0("Ib"), H("v2", h, m, 2048, 16), True, False),
                        mm(T.dif[:, 128 * w:128 * w + 128], A0("Im"), H("v2", h, m - 1, 2048, 16), False, True)]
            dx = P(fns, 1024, YK("v2", h) + ["Ib", "Im"], ["dif" + hs], acq="dif")
            A(act(H("Va", h, 512 * q, 512 * q + 512), T.dif[:, :], AF.Abs), 512, ["dif" + hs], ["Va%s%d" % (hs, q)], use=dx)
        fns = [mm(T.sm[:, 0:104], A0("w7"), A0("cpad"), True, False)]
        for w in range(12):
            fns.append(mm(T.sm[:, 12 - w:104:13], T.Vb[:, 128 * h:128 * h + 128, w] if h in EY else H("Va", h, 128 * w, 128 * w + 128), A0("G1"),
                          False, w == 11))
        tx = P(fns, 104 + 768, ["w7", "cpad", "G1"] + (["Vb%s%d" % (hs, b) for b in range(4)] if h in EY else ["Va%s%d" % (hs, q) for q in range(3)]),
               ["S" + hs], acq="sm")
        A(act(H("nx", h), T.sm[:, 0:104], AF.Relu, 26256.0, -32.0), 104, ["S" + hs], ["nx" + hs], use=tx)
        V(scan(H("ns", h), A0("ONE"), H("nx", h), Op.add, Op.min), 104, ["ONE", "nx" + hs], ["ns" + hs])
        V(cp(H("Xn", h, 0, 128, 16), H("ns", h, 12, None, 13)), 8, ["ns" + hs, "Xn" + hs], ["Xn" + hs])
        V(scan(H("Xnr", h), T.RD[:, 0:128], H("Xn", h), Op.mult, Op.add), 64, ["RD", "Xn" + hs], ["Xnr" + hs])
        tx = P([mm(T.sm[:, 0:128], A0("w7"), A0("c3"), True, False), mm(T.sm[:, 0:128], H("Xnr", h), A0("Ib"), False, True)], 256,
               ["w7", "c3", "Xnr" + hs, "Ib"], ["n" + hs], acq="sm")
        a = A(act(H("nsb", h), T.sm[:, 0:128]), 128, ["n" + hs], ["nsb" + hs], use=tx)
        zo = T.zm[:, 256 * t + 128 * h:256 * t + 128 * h + 128]
        V(tt(zo, H("zp", h), T.sm[:, 0:128], Op.add), 128, ["zp" + hs, "n" + hs], ["zm%d%d" % (t, h)], use=tx, after=[a])
        send(t, "z", h, T.zl[:, 256 * t + 128 * h:256 * t + 128 * h + 128], zo, "zm%d%d" % (t, h))
        tx = P([mm(T.sm[:, 0:32], A0("Ih"), A0("Qc"), True, False)] +
               [mm(T.sm[:, 0:32], T.Wu[:, 128 * u:128 * u + 128], H("nsb", h, u, None, 4), False, u == 3) for u in range(4)], 320,
               ["Ih", "Qc", "nsb" + hs] + ["Wu%d" % u for u in range(4)], ["Q" + hs], acq="sm")
        V(cp(H("tof", h), T.sm[:, 0:32]), 32, ["Q" + hs], ["tof" + hs], use=tx)
        to = T.ts[:, 1024 * t + 512 * h:1024 * t + 512 * h + 512]
        A(act(to, H("v2", h, 0, 2048).indirect(H("tof", h))), 512 * 1.5, YK("v2", h) + ["tof" + hs], ["ts%d%d" % (t, h)])
        send(t, "T", h, T["tl%d" % (t + 1)][:, 128 * h:128 * h + 128, :], to, "ts%d%d" % (t, h))

    for t in range(NV):
        tag[0] = ("L", 0, t)
        gatherlist(t)
        for h in range(2):
            tag[0] = ("F", h, t)
            front(t, h)
        for h in range(2):
            tag[0] = ("H", h, t)
            heavy(t, h)
            tag[0] = ("D", h, t)
            decide(t, h)
        if t < NV - 1:
            tag[0] = ("C", 0, t)
            counts(t)
        for h in range(2):
            tag[0] = ("N", h, t)
            fresh(t, h)
            tag[0] = ("E", h, t)
            finish(t, h)
    tag[0] = ("O", 0, 0)

    st = "st%d" % (NV % 2)
    V(ts(A0("li"), A0("LF"), T.al[:, 4 * NV - 4:4 * NV - 3], None, Op.subtract), 16, ["LF", "A%d" % (NV - 1)], ["li"])
    C(ts(A0("lm"), A0("li"), 255, None, Op.bitwise_and), 16, ["li"], "lm")
    C(cp(A0("lu"), A0("lm")), 16, ["lm"], "lu")
    A(act(A0("ysb"), T[st][:, :].indirect(T.lu[:, :])), 256 * 1.5, ["lu", st + "_0", st + "_1"], ["ysb"])

    def store(out, in_, rd):
        add("d", [lambda last: gs["d"].dma_start(out, in_)], 2.0, rd, [], pin=("sto", 16))
    store(T.ys[:, :], T.ysb[:, :], ["ysb"])
    for h in range(2):
        c = 256 * (NV - 1) + 128 * h
        V(ts(T.zb[:, 128 * h:128 * h + 128], T.zl[:, c:c + 128], -9.0, None, Op.add), 128, ["z%d%d" % (NV, h)], ["z0%d" % h])
        store(T.yz[:, 128 * h:128 * h + 128], T.zb[0:128:16, 128 * h:128 * h + 128], ["z0%d" % h])
    fin = []
    for h in range(2):
        for a in range(4):
            src = T["tl%d" % NV][:, 128 * h:128 * h + 128, a]
            dst = T.ytb[:, 256 * a + 128 * h:256 * a + 128 * h + 128]
            key = "yt%d%d" % (h, a)
            fin.append(key)
            if a < 2:
                V(cp(dst, src), 64, ["T%d%d" % (NV, h)], [key])
            else:
                A(act(dst, src), 128, ["T%d%d" % (NV, h)], [key])
    store(T.yt[:, :], T.ytb[:, :], fin)
    return ops


def schedule(ops):
    n = len(ops)
    succ = [[] for _ in range(n)]
    for i, o in enumerate(ops):
        for d in o["deps"]:
            succ[d].append(i)
    pr = [0.0] * n
    for i in range(n - 1, -1, -1):
        pr[i] = ops[i]["cost"] + 0.04 + max([pr[k] for k in succ[i]], default=0.0)
    pr = [pr[i] + ops[i]["bonus"] for i in range(n)]
    left = [len(o["deps"]) for o in ops]
    members = {}
    for i, o in enumerate(ops):
        if o["use"] is not None:
            members.setdefault(o["use"], []).append(i)
    ready = {e: [] for e in "vapqdn"}
    for i in range(n):
        if left[i] == 0:
            ready[ops[i]["eng"]].append(i)
    free = {e: 0.0 for e in "vapqdn"}
    end, order, holder, pend = [0.0] * n, [], {}, {}
    dep_end = [0.0] * n
    while len(order) < n:
        best = None
        for e in "vapqdn":
            cand = []
            for i in ready[e]:
                o = ops[i]
                b = o["acq"]
                est = dep_end[i]
                if b is not None and b in holder:
                    tx = holder[b]
                    if pend[tx] > 0:
                        continue
                    est = max(est, max(end[m] for m in members[tx]) + 0.04)
                if e in "vapq":
                    est = max(est, free[e])
                cand.append((est, i))
            if not cand:
                continue
            lo = min(c[0] for c in cand) + WIN
            est, i = max((c for c in cand if c[0] <= lo), key=lambda c: pr[c[1]])
            if best is None or est < best[0]:
                best = (est, i, e)
        est, i, e = best
        o = ops[i]
        ready[e].remove(i)
        if o["acq"] is not None:
            b = o["acq"]
            if b in holder:
                for m in members[holder[b]]:
                    o["deps"].setdefault(m, False)
            holder[b] = i
            pend[i] = len(members[i])
        if o["use"] is not None:
            pend[o["use"]] -= 1
        end[i] = est + o["cost"]
        if e in "vapq":
            free[e] = end[i]
        order.append((est, i))
        for k in succ[i]:
            left[k] -= 1
            dep_end[k] = max(dep_end[k], end[i] + 0.04)
            if left[k] == 0:
                ready[ops[k]["eng"]].append(k)
    return [i for _, i in order], end


def emit(ops, order, T, gs):
    lastacc = {}
    for i in order:
        if ops[i]["eng"] == "p" and ops[i]["use"] is not None:
            lastacc[ops[i]["use"]] = i
    count = {}
    done = {}
    know = {e: {} for e in "vapqd"}

    def after(e, i, raw):
        o = ops[i]
        sem, val, clk = done[i]
        if o["eng"] == e == "p" and not raw:
            return
        if know[e].get(sem, 0) >= val:
            return
        gs[e].wait_ge(T.sem[sem], val)
        for k, w in clk.items():
            if know[e].get(k, 0) < w:
                know[e][k] = w
        know[e][sem] = max(val, know[e].get(sem, 0))
    for i in order:
        o = ops[i]
        e = o["eng"]
        if e == "n":
            done[i] = (o["sym"][0], o["sym"][1], {})
            continue
        ds = sorted(o["deps"].items(), key=lambda d: -done[d[0]][1] if d[0] in done else 0)
        for d, raw in ds:
            after(e, d, raw)
        for x, fn in enumerate(o["fns"]):
            last = e == "p" and lastacc.get(o["use"]) == i and x == len(o["fns"]) - 1
            c = fn(last)
            if e in "vap" or (e == "q" and o["sym"] is None):
                c.then_inc(T.sem[e], 1)
                count[e] = count.get(e, 0) + 1
            elif e == "d":
                sem, add = o["sym"]
                c.then_inc(T.sem[sem], add)
                count[sem] = count.get(sem, 0) + add
            else:
                count["loc"] = count.get("loc", 0) + gs["neng"]
        sem = e if e in "vap" or (e == "q" and o["sym"] is None) else ("loc" if e == "q" else o["sym"][0])
        done[i] = (sem, count[sem], dict(know[e]))
    gs["d"].wait_ge(T.sem.sto, count["sto"])
    for sem in ("v", "a", "p", "q", "loc"):
        gs["q"].wait_ge(T.sem[sem], count[sem])


def rank_program(g, core, T, topo):
    rank = T.rank_of(core)
    if rank is None:
        return
    dst = T.cores[(rank + 1) % len(T.cores)]
    rid, pid, _ = topo.addr(dst)
    gs = {"v": g.vector, "a": g.scalar, "p": g.tensor, "q": g, "d": g.sync, "neng": len(topo.engines(core, dst))}
    ops = build(T, gs, (rid, pid, topo.mask(core, dst)))
    order, _ = schedule(ops)
    emit(ops, order, T, gs)
